import numpy as np
import ml_dtypes


def mxq(x, axis, fmt="e4m3"):
    dtype, down = {"e4m3": (ml_dtypes.float8_e4m3fn, 7), "e5m2": (ml_dtypes.float8_e5m2, 14)}[fmt]
    v = np.moveaxis(np.asarray(x, np.float32).astype(ml_dtypes.bfloat16).astype(np.float64), axis, -1)
    blocks = v.reshape(v.shape[:-1] + (-1, 32))
    amax = np.abs(blocks).max(-1, keepdims=True)
    byte = np.maximum(np.where(amax > 0, np.frexp(amax)[1] - 1 + 127, 0) - down, 1)
    scale = np.exp2(byte - 127.0)
    codes = (blocks / scale).astype(np.float32).astype(dtype).astype(np.float64)
    return np.moveaxis((codes * scale).reshape(v.shape), -1, axis)


WIDE = False


def mx_kscale(k):
    if not WIDE:
        return np.ones(k)
    levels = np.array([10, -10, 5, -5, 0])
    if k % 512:
        return np.exp2(np.random.permutation(np.resize(levels, k // 32))).repeat(32)
    a = np.empty((k // 512, 16))
    for p in range(k // 512):
        a[p, :8] = np.random.permutation(np.resize(levels, 8))
        for g in range(8):
            far = levels[np.abs(levels - a[p, g]) >= 10]
            a[p, g + 8] = far[np.random.randint(len(far))]
    return np.exp2(a.ravel()).repeat(32)


def f64(x):
    return np.asarray(x).astype(np.float64)


def striped(idx):
    return np.tile(idx.reshape(-1, 16).T, (8, 1)).astype(np.uint16)


def unstriped(offs):
    return offs[:16].T.reshape(-1).astype(np.int64)


def pack_weight(w):
    k, n = w.shape
    w = f64(np.asarray(w, np.float32).astype(ml_dtypes.bfloat16)).reshape(k // 32, 32, n)
    amax = np.abs(w).max(1)
    byte = np.clip(np.where(amax > 0, np.frexp(amax)[1] - 1 + 127 - 7, 1), 1, 254)
    scaled = (w * np.exp2(127.0 - byte)[:, None, :]).reshape(k, n).astype(np.float32)
    words = np.ascontiguousarray(scaled.reshape(k // 512, 128, 4, n).transpose(0, 1, 3, 2)).astype(ml_dtypes.float8_e4m3fn).view(np.uint8)
    return words, np.ascontiguousarray(byte.astype(np.uint8).reshape(k // 512, 16, n))


def unpack_weight(words, scales):
    g, p, n, _ = words.shape
    vals = np.ascontiguousarray(words).view(ml_dtypes.float8_e4m3fn).astype(np.float64) * np.repeat(np.exp2(scales.astype(np.float64) - 127.0), 8, axis=1)[..., None]
    return vals.transpose(0, 1, 3, 2).reshape(g * 512, n)


def gelu(v):
    return 0.5 * v * (1.0 + np.tanh(np.sqrt(2.0 / np.pi) * (v + 0.044715 * v**3)))


K, T, S, V, H, N = 1024, 2048, 1024, 512, 512, 128


def setup_inputs():
    n = np.random.standard_normal
    s = mx_kscale(K)[:, None]
    u = mx_kscale(H)
    packed_xT = pack_weight(n((K, T)) * s)
    packed_w3 = pack_weight(n((H, N)) / np.sqrt(H) / u[:, None])
    return {
        "x_words": packed_xT[0],
        "x_scales": packed_xT[1],
        "w1": (n((K, H)) / np.sqrt(2 * K) / s * u).astype(np.float32),
        "w2": (n((K, H)) / np.sqrt(2 * K) / s * u).astype(np.float32),
        "w3_words": packed_w3[0],
        "w3_scales": packed_w3[1],
        "offs": striped(np.random.permutation(T)[:S]),
        "cen": striped(np.random.permutation(S)[:V]),
        "pos1": striped(np.random.permutation(S)[:V]),
        "pos2": striped(np.random.permutation(S)[:V]),
    }


def reference(x_words, x_scales, w1, w2, w3_words, w3_scales, offs, cen, pos1, pos2):
    xq = unpack_weight(x_words, x_scales)[:, unstriped(offs)]
    y = mxq(f64(w1), 0, "e4m3").T @ xq
    yc = y[:, unstriped(cen)]
    e = mxq(f64(w2), 0, "e4m3").T @ xq
    z = np.maximum(gelu(yc + e[:, unstriped(pos1)]), gelu(yc + e[:, unstriped(pos2)]))
    return unpack_weight(w3_words, w3_scales).T @ mxq(z, 0, "e4m3")

@@ -1,0 +1,267 @@
+from contextlib import ExitStack
+
+import concourse.mybir as mybir
+
+K, T, S, V, H, N = 1024, 2048, 1024, 512, 512, 128
+FLOPS = 2 * (2 * K * H * S + H * N * V)
+
+F32 = mybir.dt.float32
+BF16 = mybir.dt.bfloat16
+I32 = mybir.dt.int32
+U32 = mybir.dt.uint32
+U16 = mybir.dt.uint16
+U8 = mybir.dt.uint8
+FP8X4 = mybir.dt.float8_e4m3fn_x4
+GELU = mybir.ActivationFunctionType.Gelu_apprx_tanh
+ADD = mybir.AluOpType.add
+MAX = mybir.AluOpType.max
+MULT = mybir.AluOpType.mult
+
+P = 128
+PACK = 4
+PASSES = K // (P * PACK)
+BANK = 512
+HALF_H = H // 2
+SLICES = (256, 128, 128)
+VECTOR_CASTS = (3, 5, 7)
+GPSIMD_CASTS = ()
+
+
+def tile_picked_edgecv_gelu_p_kernel(
+    tc, x_words, x_scales, w1, w2, w3_words, w3_scales, offs, cen, pos1, pos2, out
+):
+    nc = tc.nc
+    with ExitStack() as ctx:
+        keep = ctx.enter_context(tc.tile_pool(name="keep", bufs=1))
+        psum = ctx.enter_context(tc.psum_pool(name="psum", bufs=1))
+
+        def bank(index, width):
+            return psum.tile([P, width], F32, name="bank%d" % index, tag="bank%d" % index)
+
+        def sbuf(shape, dtype, name, tag=None):
+            return keep.tile(shape, dtype, name=name, tag=tag or name, align_bytes=64)
+
+        def load_list(source, name):
+            tile = keep.tile(list(source.shape), U16, name=name)
+            nc.sync.dma_start(tile[:], source)
+            return tile
+
+        pieces = [(w, g, half) for w in (w1, w2) for g in range(PASSES) for half in range(2)]
+
+        scale_table = sbuf([P, T], U8, "scale_table")
+        nc.gpsimd.memset(scale_table[:].bitcast(I32), 0)
+        offs_t = load_list(offs, "offs_t")
+        for q in range(4):
+            nc.sync.dma_start(
+                scale_table[32 * q : 32 * q + 4 * PASSES, :].bitcast(I32),
+                x_scales[:, 4 * q : 4 * q + 4, :].bitcast(I32),
+            )
+        zero_in = keep.tile([P, 1], F32, name="zero_in")
+        nc.vector.memset(zero_in[:], 0.0)
+        zero_bias = keep.tile([P, 1], F32, name="zero_bias")
+        nc.scalar.activation(zero_bias[:], zero_in[:], GELU)
+        w3_plane = sbuf([P, N], U8, "w3_plane")
+        nc.vector.memset(w3_plane[:].bitcast(I32), 0)
+
+        word_tables = [sbuf([P, T], I32, "word_table%d" % g) for g in range(PASSES)]
+        raw = [sbuf([P, PACK, HALF_H], F32, "raw%d" % n) for n in range(len(pieces))]
+
+        def load_words(g):
+            nc.sync.dma_start(word_tables[g][:], x_words[g].rearrange("p n t -> p (n t)").bitcast(I32))
+
+        def load_weights(n):
+            w, g, half = pieces[n]
+            rows = w[g * P * PACK : (g + 1) * P * PACK, half * HALF_H : (half + 1) * HALF_H]
+            nc.sync.dma_start(raw[n][:], rows.rearrange("(p j) c -> p j c", j=PACK))
+
+        load_words(0)
+        load_weights(0)
+        load_weights(1)
+        load_words(1)
+        for n in range(2, 6):
+            load_weights(n)
+        cen_t = load_list(cen, "cen_t")
+        load_weights(6)
+        load_weights(7)
+        pos_t = [load_list(pos1, "pos1_t"), load_list(pos2, "pos2_t")]
+        w3_codes = sbuf([P, N], I32, "w3_codes")
+        nc.sync.dma_start(w3_codes[:], w3_words[0].rearrange("p n t -> p (n t)").bitcast(I32))
+        for q in range(4):
+            nc.sync.dma_start(
+                w3_plane[32 * q : 32 * q + 4, :].bitcast(I32),
+                w3_scales[0, 4 * q : 4 * q + 4, :].bitcast(I32),
+            )
+
+        x_plane = sbuf([P, S], U8, "x_plane")
+        x_codes = {}
+
+        def gather_words(g, lo, hi):
+            tile = sbuf([P, hi - lo], U32, "x_codes%d_%d" % (g, lo))
+            nc.vector.tensor_copy(tile[:], word_tables[g][:].bitcast(U32).indirect(offs_t[:, lo // 16 : hi // 16]))
+            for h in range(lo // BANK, hi // BANK):
+                x_codes[g, h] = tile[:, h * BANK - lo : (h + 1) * BANK - lo]
+
+        w_bf = [sbuf([P, PACK, P, PACK], BF16, "w_bf%d" % r) for r in range(2 * PASSES)]
+        w_codes = {}
+        w_plane = {}
+
+        def cast(n):
+            half = n % 2
+            dst = w_bf[n // 2][:, :, half * 64 : (half + 1) * 64, :].rearrange("p (u e) m j -> p u m j e", e=2)
+            src = raw[n][:].rearrange("p j (m u e) -> p u m j e", u=2, e=2)
+            if n in VECTOR_CASTS:
+                nc.vector.tensor_copy(dst, src)
+            elif n in GPSIMD_CASTS:
+                for u in range(2):
+                    nc.gpsimd.tensor_scalar(dst[:, u], src[:, u], 1.0, 0.0, MULT, ADD)
+            else:
+                nc.scalar.copy(dst, src)
+
+        def quantise(r):
+            for u in range(2):
+                w_codes[r, u] = sbuf([P, 2 * P], U32, "w_codes%d_%d" % (r, u))
+                w_plane[r, u] = sbuf([P, 2 * P], U8, "w_plane%d_%d" % (r, u))
+                nc.vector.quantize_mx(
+                    out=w_codes[r, u][:].bitcast(FP8X4),
+                    scales=w_plane[r, u][:],
+                    in_=w_bf[r][:, 2 * u : 2 * u + 2].rearrange("p t m j -> p (t m j)"),
+                )
+
+        accs = {}
+        results = {}
+
+        def multiply(w, t, g):
+            for h in range(2):
+                if g == 0:
+                    accs[w, t, h] = bank(2 * t + h, BANK)
+                cols = slice((t % 2) * P, (t % 2 + 1) * P)
+                nc.tensor.matmul_mx(
+                    out=accs[w, t, h][:],
+                    lhsT=w_codes[PASSES * w + g, t // 2][:, cols].bitcast(FP8X4),
+                    lhsT_scale=w_plane[PASSES * w + g, t // 2][:, cols],
+                    rhs=x_codes[g, h].bitcast(FP8X4),
+                    rhs_scale=x_plane[4 * g :, h * BANK : (h + 1) * BANK],
+                    start=(g == 0),
+                    stop=(g == PASSES - 1),
+                )
+
+        def evacuate(w, t, tag=None):
+            results[w, t] = sbuf([P, S], F32, "result%d_%d" % (w, t), tag)
+            for h in range(2):
+                nc.scalar.copy(results[w, t][:, h * BANK : (h + 1) * BANK], accs[w, t, h][:])
+
+        starts = [sum(SLICES[:s]) for s in range(len(SLICES))]
+        centres = {}
+
+        def gather_centres(t, tag=None):
+            tile = sbuf([P, V], F32, "centre%d" % t, tag)
+            nc.vector.tensor_copy(tile[:], results[0, t][:].indirect(cen_t[:]))
+            for s, width in enumerate(SLICES):
+                centres[t, s] = tile[:, starts[s] : starts[s] + width]
+
+        def gather_centres_by_slice(t):
+            for s, width in enumerate(SLICES):
+                tile = sbuf([P, width], F32, "centre%d_%d" % (t, s))
+                lists = cen_t[:, starts[s] // 16 : (starts[s] + width) // 16]
+                nc.vector.tensor_copy(tile[:], results[0, t][:].indirect(lists))
+                centres[t, s] = tile[:]
+
+        sums = {}
+        tags = {}
+        acts = {}
+
+        def open_sums(s):
+            for d in range(2):
+                if s == 0:
+                    tags[s, d] = "sum0_%d" % d
+                elif d == 0:
+                    tags[s, d] = "centre%d_%d" % (PACK - 1, s - 1)
+                else:
+                    tags[s, d] = tags[s - 1, 0]
+                sums[s, d] = sbuf([P, PACK, SLICES[s]], F32, "sum%d_%d" % (s, d), tags[s, d])
+
+        def add_neighbours(s, d, t):
+            lists = pos_t[d][:, starts[s] // 16 : (starts[s] + SLICES[s]) // 16]
+            nc.vector.tensor_tensor(sums[s, d][:, t, :], results[1, t][:].indirect(lists), centres[t, s], ADD)
+
+        def activate(s, d):
+            acts[s, d] = sbuf([P, SLICES[s], PACK], BF16, "act%d_%d" % (s, d))
+            nc.scalar.activation(
+                acts[s, d][:].rearrange("p (a i) t -> p a t i", i=4),
+                sums[s, d][:].rearrange("p t (a i) -> p a t i", i=4),
+                GELU,
+                bias=zero_bias[:],
+            )
+
+        def project(s):
+            width = SLICES[s]
+            z_bf = sbuf([P, width * PACK], BF16, "z_bf%d" % s)
+            nc.vector.tensor_tensor(
+                z_bf[:],
+                acts[s, 0][:].rearrange("p v t -> p (v t)"),
+                acts[s, 1][:].rearrange("p v t -> p (v t)"),
+                MAX,
+            )
+            z_codes = sbuf([P, width], U32, "z_codes%d" % s)
+            z_plane = sbuf([P, width], U8, "z_plane%d" % s)
+            nc.vector.quantize_mx(out=z_codes[:].bitcast(FP8X4), scales=z_plane[:], in_=z_bf[:])
+            acc = bank(s, width)
+            nc.tensor.matmul_mx(
+                out=acc[:],
+                lhsT=w3_codes[:].bitcast(FP8X4),
+                lhsT_scale=w3_plane[:],
+                rhs=z_codes[:].bitcast(FP8X4),
+                rhs_scale=z_plane[:],
+                start=True,
+                stop=True,
+            )
+            staged = sbuf([P, width], F32, "staged%d" % s)
+            nc.scalar.copy(staged[:], acc[:])
+            nc.sync.dma_start(out[:, starts[s] : starts[s] + width], staged[:])
+
+        nc.vector.tensor_copy(x_plane[:], scale_table[:].indirect(offs_t[:]))
+        gather_words(0, 0, S)
+        cast(0)
+        cast(1)
+        quantise(0)
+        gather_words(1, 0, BANK)
+        gather_words(1, BANK, S)
+        for t in range(PACK):
+            multiply(0, t, 0)
+        cast(2)
+        cast(3)
+        quantise(1)
+        cast(4)
+        cast(5)
+        for t in range(PACK):
+            multiply(0, t, 1)
+        evacuate(0, 0)
+        quantise(2)
+        gather_centres(0)
+        cast(6)
+        cast(7)
+        quantise(3)
+        evacuate(0, 1, "raw6")
+        gather_centres(1, "raw7")
+        evacuate(0, 2)
+        gather_centres(2, "w_bf3")
+        evacuate(0, 3)
+        gather_centres_by_slice(3)
+        open_sums(0)
+        for t in range(PACK):
+            for g in range(PASSES):
+                multiply(1, t, g)
+            evacuate(1, t)
+            for d in range(2):
+                add_neighbours(0, d, t)
+        for s in range(len(SLICES)):
+            if s > 0:
+                open_sums(s)
+            for d in range(2):
+                if s > 0:
+                    for t in range(PACK):
+                        add_neighbours(s, d, t)
+                activate(s, d)
+            if s > 0:
+                project(s - 1)
+        project(len(SLICES) - 1)

@@ -15,16 +15,15 @@ FP8X4 = mybir.dt.float8_e4m3fn_x4
 GELU = mybir.ActivationFunctionType.Gelu_apprx_tanh
 ADD = mybir.AluOpType.add
 MAX = mybir.AluOpType.max
-MULT = mybir.AluOpType.mult
 
 P = 128
 PACK = 4
 PASSES = K // (P * PACK)
 BANK = 512
 HALF_H = H // 2
-SLICES = (256, 128, 128)
-VECTOR_CASTS = (3, 5, 7)
-GPSIMD_CASTS = ()
+SLICES = (384, 128)
+BLOCKS = ((0, 0, 256), (0, 256, 128), (1, 0, 128))
+CAST_ENGINES = "VSBSBSVB"
 
 
 def tile_picked_edgecv_gelu_p_kernel(
@@ -46,11 +45,12 @@ def tile_picked_edgecv_gelu_p_kernel(
             nc.sync.dma_start(tile[:], source)
             return tile
 
-        pieces = [(w, g, half) for w in (w1, w2) for g in range(PASSES) for half in range(2)]
+        rounds = [(w, g) for w in (w1, w2) for g in range(PASSES)]
 
         scale_table = sbuf([P, T], U8, "scale_table")
         nc.gpsimd.memset(scale_table[:].bitcast(I32), 0)
         offs_t = load_list(offs, "offs_t")
+        pos_t = [load_list(pos1, "pos1_t")]
         for q in range(4):
             nc.sync.dma_start(
                 scale_table[32 * q : 32 * q + 4 * PASSES, :].bitcast(I32),
@@ -64,26 +64,25 @@ def tile_picked_edgecv_gelu_p_kernel(
         nc.vector.memset(w3_plane[:].bitcast(I32), 0)
 
         word_tables = [sbuf([P, T], I32, "word_table%d" % g) for g in range(PASSES)]
-        raw = [sbuf([P, PACK, HALF_H], F32, "raw%d" % n) for n in range(len(pieces))]
+        raw = {}
 
         def load_words(g):
             nc.sync.dma_start(word_tables[g][:], x_words[g].rearrange("p n t -> p (n t)").bitcast(I32))
 
-        def load_weights(n):
-            w, g, half = pieces[n]
-            rows = w[g * P * PACK : (g + 1) * P * PACK, half * HALF_H : (half + 1) * HALF_H]
-            nc.sync.dma_start(raw[n][:], rows.rearrange("(p j) c -> p j c", j=PACK))
+        def load_weights(r):
+            w, g = rounds[r]
+            raw[r] = sbuf([P, PACK, H], F32, "raw%d" % r)
+            rows = w[g * P * PACK : (g + 1) * P * PACK, :]
+            nc.sync.dma_start(raw[r][:], rows.rearrange("(p j) c -> p j c", j=PACK))
 
         load_words(0)
         load_weights(0)
-        load_weights(1)
         load_words(1)
-        for n in range(2, 6):
-            load_weights(n)
+        load_weights(1)
+        load_weights(2)
         cen_t = load_list(cen, "cen_t")
-        load_weights(6)
-        load_weights(7)
-        pos_t = [load_list(pos1, "pos1_t"), load_list(pos2, "pos2_t")]
+        load_weights(3)
+        pos_t.append(load_list(pos2, "pos2_t"))
         w3_codes = sbuf([P, N], I32, "w3_codes")
         nc.sync.dma_start(w3_codes[:], w3_words[0].rearrange("p n t -> p (n t)").bitcast(I32))
         for q in range(4):
@@ -101,31 +100,36 @@ def tile_picked_edgecv_gelu_p_kernel(
             for h in range(lo // BANK, hi // BANK):
                 x_codes[g, h] = tile[:, h * BANK - lo : (h + 1) * BANK - lo]
 
-        w_bf = [sbuf([P, PACK, P, PACK], BF16, "w_bf%d" % r) for r in range(2 * PASSES)]
+        w_bf = {}
         w_codes = {}
         w_plane = {}
 
-        def cast(n):
-            half = n % 2
-            dst = w_bf[n // 2][:, :, half * 64 : (half + 1) * 64, :].rearrange("p (u e) m j -> p u m j e", e=2)
-            src = raw[n][:].rearrange("p j (m u e) -> p u m j e", u=2, e=2)
-            if n in VECTOR_CASTS:
-                nc.vector.tensor_copy(dst, src)
-            elif n in GPSIMD_CASTS:
-                for u in range(2):
-                    nc.gpsimd.tensor_scalar(dst[:, u], src[:, u], 1.0, 0.0, MULT, ADD)
-            else:
-                nc.scalar.copy(dst, src)
-
-        def quantise(r):
+        def cast(r):
             for u in range(2):
-                w_codes[r, u] = sbuf([P, 2 * P], U32, "w_codes%d_%d" % (r, u))
-                w_plane[r, u] = sbuf([P, 2 * P], U8, "w_plane%d_%d" % (r, u))
+                w_bf[r, u] = sbuf([P, 2, P, PACK], BF16, "w_bf%d_%d" % (r, u))
+                src = raw[r][:].rearrange("p j (m u e) -> p u m j e", u=2, e=2)[:, u]
+                dst = w_bf[r, u][:].rearrange("p e m j -> p m j e")
+                engines = CAST_ENGINES[2 * r + u]
+                if engines == "V":
+                    nc.vector.tensor_copy(dst, src)
+                elif engines == "S":
+                    nc.scalar.copy(dst, src)
+                else:
+                    nc.vector.tensor_copy(dst[:, : P // 2], src[:, : P // 2])
+                    nc.scalar.copy(dst[:, P // 2 :], src[:, P // 2 :])
+
+        def quantise(r, groups):
+            for ts in groups:
+                codes = sbuf([P, len(ts) * P], U32, "w_codes%d_%d" % (r, ts[0]))
+                plane = sbuf([P, len(ts) * P], U8, "w_plane%d_%d" % (r, ts[0]))
                 nc.vector.quantize_mx(
-                    out=w_codes[r, u][:].bitcast(FP8X4),
-                    scales=w_plane[r, u][:],
-                    in_=w_bf[r][:, 2 * u : 2 * u + 2].rearrange("p t m j -> p (t m j)"),
+                    out=codes[:].bitcast(FP8X4),
+                    scales=plane[:],
+                    in_=w_bf[r, ts[0] // 2][:, ts[0] % 2 : ts[-1] % 2 + 1].rearrange("p t m j -> p (t m j)"),
                 )
+                for a, t in enumerate(ts):
+                    w_codes[r, t] = codes[:, a * P : (a + 1) * P]
+                    w_plane[r, t] = plane[:, a * P : (a + 1) * P]
 
         accs = {}
         results = {}
@@ -134,21 +138,24 @@ def tile_picked_edgecv_gelu_p_kernel(
             for h in range(2):
                 if g == 0:
                     accs[w, t, h] = bank(2 * t + h, BANK)
-                cols = slice((t % 2) * P, (t % 2 + 1) * P)
                 nc.tensor.matmul_mx(
                     out=accs[w, t, h][:],
-                    lhsT=w_codes[PASSES * w + g, t // 2][:, cols].bitcast(FP8X4),
-                    lhsT_scale=w_plane[PASSES * w + g, t // 2][:, cols],
+                    lhsT=w_codes[PASSES * w + g, t].bitcast(FP8X4),
+                    lhsT_scale=w_plane[PASSES * w + g, t],
                     rhs=x_codes[g, h].bitcast(FP8X4),
                     rhs_scale=x_plane[4 * g :, h * BANK : (h + 1) * BANK],
                     start=(g == 0),
                     stop=(g == PASSES - 1),
                 )
 
-        def evacuate(w, t, tag=None):
+        def evacuate(w, t, tag=None, shared=False):
             results[w, t] = sbuf([P, S], F32, "result%d_%d" % (w, t), tag)
             for h in range(2):
-                nc.scalar.copy(results[w, t][:, h * BANK : (h + 1) * BANK], accs[w, t, h][:])
+                target = results[w, t][:, h * BANK : (h + 1) * BANK]
+                if shared and h == 1:
+                    nc.vector.tensor_copy(target, accs[w, t, h][:])
+                else:
+                    nc.scalar.copy(target, accs[w, t, h][:])
 
         starts = [sum(SLICES[:s]) for s in range(len(SLICES))]
         centres = {}
@@ -193,19 +200,20 @@ def tile_picked_edgecv_gelu_p_kernel(
                 bias=zero_bias[:],
             )
 
-        def project(s):
-            width = SLICES[s]
-            z_bf = sbuf([P, width * PACK], BF16, "z_bf%d" % s)
+        def project(b, tag=None):
+            s, lo, width = BLOCKS[b]
+            first = starts[s] + lo
+            z_bf = sbuf([P, width * PACK], BF16, "z_bf%d" % b, tag)
             nc.vector.tensor_tensor(
                 z_bf[:],
-                acts[s, 0][:].rearrange("p v t -> p (v t)"),
-                acts[s, 1][:].rearrange("p v t -> p (v t)"),
+                acts[s, 0][:, lo : lo + width].rearrange("p v t -> p (v t)"),
+                acts[s, 1][:, lo : lo + width].rearrange("p v t -> p (v t)"),
                 MAX,
             )
-            z_codes = sbuf([P, width], U32, "z_codes%d" % s)
-            z_plane = sbuf([P, width], U8, "z_plane%d" % s)
+            z_codes = sbuf([P, width], U32, "z_codes%d" % b)
+            z_plane = sbuf([P, width], U8, "z_plane%d" % b)
             nc.vector.quantize_mx(out=z_codes[:].bitcast(FP8X4), scales=z_plane[:], in_=z_bf[:])
-            acc = bank(s, width)
+            acc = bank(b, width)
             nc.tensor.matmul_mx(
                 out=acc[:],
                 lhsT=w3_codes[:].bitcast(FP8X4),
@@ -215,36 +223,33 @@ def tile_picked_edgecv_gelu_p_kernel(
                 start=True,
                 stop=True,
             )
-            staged = sbuf([P, width], F32, "staged%d" % s)
+            staged = sbuf([P, width], F32, "staged%d" % b)
             nc.scalar.copy(staged[:], acc[:])
-            nc.sync.dma_start(out[:, starts[s] : starts[s] + width], staged[:])
+            nc.sync.dma_start(out[:, first : first + width], staged[:])
 
+        pairs = ((0, 1), (2, 3))
         nc.vector.tensor_copy(x_plane[:], scale_table[:].indirect(offs_t[:]))
         gather_words(0, 0, S)
         cast(0)
-        cast(1)
-        quantise(0)
+        quantise(0, pairs)
         gather_words(1, 0, BANK)
         gather_words(1, BANK, S)
         for t in range(PACK):
             multiply(0, t, 0)
+        cast(1)
+        quantise(1, ((0,), (1,), (2, 3)))
         cast(2)
-        cast(3)
-        quantise(1)
-        cast(4)
-        cast(5)
         for t in range(PACK):
             multiply(0, t, 1)
-        evacuate(0, 0)
-        quantise(2)
+        evacuate(0, 0, None, True)
+        quantise(2, pairs)
         gather_centres(0)
-        cast(6)
-        cast(7)
-        quantise(3)
-        evacuate(0, 1, "raw6")
-        gather_centres(1, "raw7")
+        cast(3)
+        quantise(3, pairs)
+        evacuate(0, 1)
+        gather_centres(1)
         evacuate(0, 2)
-        gather_centres(2, "w_bf3")
+        gather_centres(2)
         evacuate(0, 3)
         gather_centres_by_slice(3)
         open_sums(0)
@@ -262,6 +267,5 @@ def tile_picked_edgecv_gelu_p_kernel(
                     for t in range(PACK):
                         add_neighbours(s, d, t)
                 activate(s, d)
-            if s > 0:
-                project(s - 1)
-        project(len(SLICES) - 1)
+        for b in range(len(BLOCKS)):
+            project(b)

@@ -20,10 +20,7 @@ P = 128
 PACK = 4
 PASSES = K // (P * PACK)
 BANK = 512
-HALF_H = H // 2
-SLICES = (384, 128)
-BLOCKS = ((0, 0, 256), (0, 256, 128), (1, 0, 128))
-CAST_ENGINES = "VSBSBSVB"
+SLICES = (256, 128, 128)
 
 
 def tile_picked_edgecv_gelu_p_kernel(
@@ -48,9 +45,16 @@ def tile_picked_edgecv_gelu_p_kernel(
         rounds = [(w, g) for w in (w1, w2) for g in range(PASSES)]
 
         scale_table = sbuf([P, T], U8, "scale_table")
-        nc.gpsimd.memset(scale_table[:].bitcast(I32), 0)
+        nc.vector.memset(scale_table[:, : T // 2].bitcast(I32), 0)
+        nc.gpsimd.memset(scale_table[:, T // 2 :].bitcast(I32), 0)
         offs_t = load_list(offs, "offs_t")
-        pos_t = [load_list(pos1, "pos1_t")]
+        word_tables = [sbuf([P, T], I32, "word_table%d" % g) for g in range(PASSES)]
+
+        def load_words(g, lo, hi):
+            words = x_words[g].rearrange("p n t -> p (n t)").bitcast(I32)
+            nc.sync.dma_start(word_tables[g][:, lo:hi], words[:, lo:hi])
+
+        load_words(0, 0, 3 * T // 8)
         for q in range(4):
             nc.sync.dma_start(
                 scale_table[32 * q : 32 * q + 4 * PASSES, :].bitcast(I32),
@@ -63,11 +67,7 @@ def tile_picked_edgecv_gelu_p_kernel(
         w3_plane = sbuf([P, N], U8, "w3_plane")
         nc.vector.memset(w3_plane[:].bitcast(I32), 0)
 
-        word_tables = [sbuf([P, T], I32, "word_table%d" % g) for g in range(PASSES)]
         raw = {}
-
-        def load_words(g):
-            nc.sync.dma_start(word_tables[g][:], x_words[g].rearrange("p n t -> p (n t)").bitcast(I32))
 
         def load_weights(r):
             w, g = rounds[r]
@@ -75,14 +75,14 @@ def tile_picked_edgecv_gelu_p_kernel(
             rows = w[g * P * PACK : (g + 1) * P * PACK, :]
             nc.sync.dma_start(raw[r][:], rows.rearrange("(p j) c -> p j c", j=PACK))
 
-        load_words(0)
+        load_words(0, 3 * T // 8, T)
         load_weights(0)
-        load_words(1)
+        load_words(1, 0, T)
         load_weights(1)
-        load_weights(2)
         cen_t = load_list(cen, "cen_t")
+        load_weights(2)
         load_weights(3)
-        pos_t.append(load_list(pos2, "pos2_t"))
+        pos_t = [load_list(pos1, "pos1_t"), load_list(pos2, "pos2_t")]
         w3_codes = sbuf([P, N], I32, "w3_codes")
         nc.sync.dma_start(w3_codes[:], w3_words[0].rearrange("p n t -> p (n t)").bitcast(I32))
         for q in range(4):
@@ -104,19 +104,14 @@ def tile_picked_edgecv_gelu_p_kernel(
         w_codes = {}
         w_plane = {}
 
-        def cast(r):
-            for u in range(2):
-                w_bf[r, u] = sbuf([P, 2, P, PACK], BF16, "w_bf%d_%d" % (r, u))
-                src = raw[r][:].rearrange("p j (m u e) -> p u m j e", u=2, e=2)[:, u]
-                dst = w_bf[r, u][:].rearrange("p e m j -> p m j e")
-                engines = CAST_ENGINES[2 * r + u]
-                if engines == "V":
-                    nc.vector.tensor_copy(dst, src)
-                elif engines == "S":
-                    nc.scalar.copy(dst, src)
-                else:
-                    nc.vector.tensor_copy(dst[:, : P // 2], src[:, : P // 2])
-                    nc.scalar.copy(dst[:, P // 2 :], src[:, P // 2 :])
+        def cast(r, u, on_vector, tag=None):
+            w_bf[r, u] = sbuf([P, 2, P, PACK], BF16, "w_bf%d_%d" % (r, u), tag)
+            src = raw[r][:].rearrange("p j (m u e) -> p u m j e", u=2, e=2)[:, u]
+            dst = w_bf[r, u][:].rearrange("p e m j -> p m j e")
+            if on_vector > 0:
+                nc.vector.tensor_copy(dst[:, :on_vector], src[:, :on_vector])
+            if on_vector < P:
+                nc.scalar.copy(dst[:, on_vector:], src[:, on_vector:])
 
         def quantise(r, groups):
             for ts in groups:
@@ -161,59 +156,47 @@ def tile_picked_edgecv_gelu_p_kernel(
         centres = {}
 
         def gather_centres(t, tag=None):
-            tile = sbuf([P, V], F32, "centre%d" % t, tag)
-            nc.vector.tensor_copy(tile[:], results[0, t][:].indirect(cen_t[:]))
-            for s, width in enumerate(SLICES):
-                centres[t, s] = tile[:, starts[s] : starts[s] + width]
+            centres[t] = sbuf([P, V], F32, "centre%d" % t, tag)
+            nc.vector.tensor_copy(centres[t][:], results[0, t][:].indirect(cen_t[:]))
 
-        def gather_centres_by_slice(t):
-            for s, width in enumerate(SLICES):
-                tile = sbuf([P, width], F32, "centre%d_%d" % (t, s))
-                lists = cen_t[:, starts[s] // 16 : (starts[s] + width) // 16]
-                nc.vector.tensor_copy(tile[:], results[0, t][:].indirect(lists))
-                centres[t, s] = tile[:]
+        first_sums = [sbuf([P, 2, V], F32, "first_sum%d" % d) for d in range(2)]
+        last_sums = [sbuf([P, 2, V], F32, "last_sum%d" % d) for d in range(2)]
+        acts = {
+            (s, d): sbuf([P, 2, width, 2], BF16, "act%d_%d" % (s, d)) for s, width in enumerate(SLICES) for d in range(2)
+        }
 
-        sums = {}
-        tags = {}
-        acts = {}
+        def add_neighbours(t, d):
+            nc.vector.tensor_tensor((first_sums if t < 2 else last_sums)[d][:, t % 2, :], results[1, t][:].indirect(pos_t[d][:]), centres[t][:], ADD)
 
-        def open_sums(s):
-            for d in range(2):
-                if s == 0:
-                    tags[s, d] = "sum0_%d" % d
-                elif d == 0:
-                    tags[s, d] = "centre%d_%d" % (PACK - 1, s - 1)
-                else:
-                    tags[s, d] = tags[s - 1, 0]
-                sums[s, d] = sbuf([P, PACK, SLICES[s]], F32, "sum%d_%d" % (s, d), tags[s, d])
-
-        def add_neighbours(s, d, t):
-            lists = pos_t[d][:, starts[s] // 16 : (starts[s] + SLICES[s]) // 16]
-            nc.vector.tensor_tensor(sums[s, d][:, t, :], results[1, t][:].indirect(lists), centres[t, s], ADD)
-
-        def activate(s, d):
-            acts[s, d] = sbuf([P, SLICES[s], PACK], BF16, "act%d_%d" % (s, d))
-            nc.scalar.activation(
-                acts[s, d][:].rearrange("p (a i) t -> p a t i", i=4),
-                sums[s, d][:].rearrange("p t (a i) -> p a t i", i=4),
-                GELU,
-                bias=zero_bias[:],
+        def add_neighbours_of_slice(t, s, d):
+            lo, hi = starts[s], starts[s] + SLICES[s]
+            nc.vector.tensor_tensor(
+                last_sums[d][:, t - 2, lo:hi],
+                results[1, t][:].indirect(pos_t[d][:, lo // 16 : hi // 16]),
+                centres[t][:, lo:hi],
+                ADD,
             )
 
-        def project(b, tag=None):
-            s, lo, width = BLOCKS[b]
-            first = starts[s] + lo
-            z_bf = sbuf([P, width * PACK], BF16, "z_bf%d" % b, tag)
+        def activate(u, s, d):
+            lo, hi = starts[s], starts[s] + SLICES[s]
+            source = (first_sums if u == 0 else last_sums)[d][:, :, lo:hi]
+            nc.scalar.activation(acts[s, d][:, u], source.rearrange("p e v -> p v e"), GELU, bias=zero_bias[:])
+
+        def project(s):
+            width = SLICES[s]
+            z_bf = sbuf([P, width, 2, 2], BF16, "z_bf%d" % s)
             nc.vector.tensor_tensor(
                 z_bf[:],
-                acts[s, 0][:, lo : lo + width].rearrange("p v t -> p (v t)"),
-                acts[s, 1][:, lo : lo + width].rearrange("p v t -> p (v t)"),
+                acts[s, 0][:].rearrange("p u v e -> p v u e"),
+                acts[s, 1][:].rearrange("p u v e -> p v u e"),
                 MAX,
             )
-            z_codes = sbuf([P, width], U32, "z_codes%d" % b)
-            z_plane = sbuf([P, width], U8, "z_plane%d" % b)
-            nc.vector.quantize_mx(out=z_codes[:].bitcast(FP8X4), scales=z_plane[:], in_=z_bf[:])
-            acc = bank(b, width)
+            z_codes = sbuf([P, width], U32, "z_codes%d" % s)
+            z_plane = sbuf([P, width], U8, "z_plane%d" % s)
+            nc.vector.quantize_mx(
+                out=z_codes[:].bitcast(FP8X4), scales=z_plane[:], in_=z_bf[:].rearrange("p v u e -> p (v u e)")
+            )
+            acc = bank(s, width)
             nc.tensor.matmul_mx(
                 out=acc[:],
                 lhsT=w3_codes[:].bitcast(FP8X4),
@@ -223,49 +206,63 @@ def tile_picked_edgecv_gelu_p_kernel(
                 start=True,
                 stop=True,
             )
-            staged = sbuf([P, width], F32, "staged%d" % b)
+            staged = sbuf([P, width], F32, "staged%d" % s)
             nc.scalar.copy(staged[:], acc[:])
-            nc.sync.dma_start(out[:, first : first + width], staged[:])
+            nc.sync.dma_start(out[:, starts[s] : starts[s] + width], staged[:])
 
-        pairs = ((0, 1), (2, 3))
         nc.vector.tensor_copy(x_plane[:], scale_table[:].indirect(offs_t[:]))
         gather_words(0, 0, S)
-        cast(0)
-        quantise(0, pairs)
+        for u in range(2):
+            cast(0, u, u * P // 2)
+            quantise(0, ((2 * u, 2 * u + 1),))
         gather_words(1, 0, BANK)
         gather_words(1, BANK, S)
         for t in range(PACK):
             multiply(0, t, 0)
-        cast(1)
-        quantise(1, ((0,), (1,), (2, 3)))
-        cast(2)
+        cast(1, 0, P // 2)
+        quantise(1, ((0,), (1,)))
+        cast(1, 1, 0)
+        quantise(1, ((2, 3),))
         for t in range(PACK):
             multiply(0, t, 1)
         evacuate(0, 0, None, True)
-        quantise(2, pairs)
         gather_centres(0)
-        cast(3)
-        quantise(3, pairs)
         evacuate(0, 1)
         gather_centres(1)
-        evacuate(0, 2)
-        gather_centres(2)
-        evacuate(0, 3)
-        gather_centres_by_slice(3)
-        open_sums(0)
-        for t in range(PACK):
+        cast(2, 0, 0, "w_codes1_1")
+        quantise(2, ((0, 1),))
+        cast(3, 0, P)
+        quantise(3, ((0, 1),))
+        for t in (2, 3):
+            evacuate(0, t)
+            gather_centres(t, "w_bf3_0" if t == 2 else None)
+        cast(2, 1, 0, "w_plane1_1")
+        quantise(2, ((2, 3),))
+        for t in (0, 1):
+            for g in range(PASSES):
+                multiply(1, t, g)
+        evacuate(1, 0)
+        for d in range(2):
+            add_neighbours(0, d)
+        cast(3, 1, 0, "w_codes3_0")
+        quantise(3, ((2, 3),))
+        evacuate(1, 1)
+        for d in range(2):
+            add_neighbours(1, d)
+        for t in (2, 3):
             for g in range(PASSES):
                 multiply(1, t, g)
             evacuate(1, t)
-            for d in range(2):
-                add_neighbours(0, d, t)
+        for d in range(2):
+            for s in range(len(SLICES)):
+                activate(0, s, d)
+        for d in range(2):
+            add_neighbours(2, d)
         for s in range(len(SLICES)):
-            if s > 0:
-                open_sums(s)
             for d in range(2):
-                if s > 0:
-                    for t in range(PACK):
-                        add_neighbours(s, d, t)
-                activate(s, d)
-        for b in range(len(BLOCKS)):
-            project(b)
+                add_neighbours_of_slice(3, s, d)
+        for s in range(len(SLICES)):
+            for d in range(2):
+                activate(1, s, d)
+        for s in range(len(SLICES)):
+            project(s)

@@ -30,11 +30,15 @@ def tile_picked_edgecv_gelu_p_kernel(
     with ExitStack() as ctx:
         keep = ctx.enter_context(tc.tile_pool(name="keep", bufs=1))
         psum = ctx.enter_context(tc.psum_pool(name="psum", bufs=1))
+        reused = ctx.enter_context(tc.tile_pool(name="reused", bufs=1))
+        places = {"centre2": 0, "w_bf3_0": 1024, "result0_3": 2048}
 
         def bank(index, width):
             return psum.tile([P, width], F32, name="bank%d" % index, tag="bank%d" % index)
 
         def sbuf(shape, dtype, name, tag=None):
+            if name in places:
+                return reused.tile(shape, dtype, name=name, tag=name, align_bytes=64, offset=places[name])
             return keep.tile(shape, dtype, name=name, tag=tag or name, align_bytes=64)
 
         def load_list(source, name):
@@ -79,8 +83,8 @@ def tile_picked_edgecv_gelu_p_kernel(
         load_weights(0)
         load_words(1, 0, T)
         load_weights(1)
-        cen_t = load_list(cen, "cen_t")
         load_weights(2)
+        cen_t = load_list(cen, "cen_t")
         load_weights(3)
         pos_t = [load_list(pos1, "pos1_t"), load_list(pos2, "pos2_t")]
         w3_codes = sbuf([P, N], I32, "w3_codes")
@@ -104,18 +108,20 @@ def tile_picked_edgecv_gelu_p_kernel(
         w_codes = {}
         w_plane = {}
 
-        def cast(r, u, on_vector, tag=None):
-            w_bf[r, u] = sbuf([P, 2, P, PACK], BF16, "w_bf%d_%d" % (r, u), tag)
+        def cast(r, u, copy, lo=0, hi=P, tag=None):
+            if (r, u) not in w_bf:
+                w_bf[r, u] = sbuf([P, 2, P, PACK], BF16, "w_bf%d_%d" % (r, u), tag)
             src = raw[r][:].rearrange("p j (m u e) -> p u m j e", u=2, e=2)[:, u]
             dst = w_bf[r, u][:].rearrange("p e m j -> p m j e")
-            if on_vector > 0:
-                nc.vector.tensor_copy(dst[:, :on_vector], src[:, :on_vector])
-            if on_vector < P:
-                nc.scalar.copy(dst[:, on_vector:], src[:, on_vector:])
+            copy(dst[:, lo:hi], src[:, lo:hi])
 
-        def quantise(r, groups):
+        def cast_shared(r, u, on_vector):
+            cast(r, u, nc.vector.tensor_copy, 0, on_vector)
+            cast(r, u, nc.scalar.copy, on_vector, P)
+
+        def quantise(r, groups, tag=None):
             for ts in groups:
-                codes = sbuf([P, len(ts) * P], U32, "w_codes%d_%d" % (r, ts[0]))
+                codes = sbuf([P, len(ts) * P], U32, "w_codes%d_%d" % (r, ts[0]), tag)
                 plane = sbuf([P, len(ts) * P], U8, "w_plane%d_%d" % (r, ts[0]))
                 nc.vector.quantize_mx(
                     out=codes[:].bitcast(FP8X4),
@@ -129,35 +135,38 @@ def tile_picked_edgecv_gelu_p_kernel(
         accs = {}
         results = {}
 
-        def multiply(w, t, g):
-            for h in range(2):
-                if g == 0:
-                    accs[w, t, h] = bank(2 * t + h, BANK)
-                nc.tensor.matmul_mx(
-                    out=accs[w, t, h][:],
-                    lhsT=w_codes[PASSES * w + g, t].bitcast(FP8X4),
-                    lhsT_scale=w_plane[PASSES * w + g, t],
-                    rhs=x_codes[g, h].bitcast(FP8X4),
-                    rhs_scale=x_plane[4 * g :, h * BANK : (h + 1) * BANK],
-                    start=(g == 0),
-                    stop=(g == PASSES - 1),
-                )
+        first_bank = {(0, 0): 0, (0, 1): 4, (0, 2): 6, (0, 3): 0, (1, 0): 2, (1, 1): 4, (1, 2): 6, (1, 3): 0}
 
-        def evacuate(w, t, tag=None, shared=False):
-            results[w, t] = sbuf([P, S], F32, "result%d_%d" % (w, t), tag)
-            for h in range(2):
-                target = results[w, t][:, h * BANK : (h + 1) * BANK]
-                if shared and h == 1:
-                    nc.vector.tensor_copy(target, accs[w, t, h][:])
-                else:
-                    nc.scalar.copy(target, accs[w, t, h][:])
+        def multiply(w, t, passes):
+            width = BANK // 2 if (w, t) == (0, 0) else BANK
+            for piece in range(S // width):
+                h, lo = divmod(piece * width, BANK)
+                for g in passes:
+                    start = (w, t, piece) not in accs
+                    if start:
+                        accs[w, t, piece] = bank(first_bank[w, t] + piece, width)
+                    nc.tensor.matmul_mx(
+                        out=accs[w, t, piece][:],
+                        lhsT=w_codes[PASSES * w + g, t].bitcast(FP8X4),
+                        lhsT_scale=w_plane[PASSES * w + g, t],
+                        rhs=x_codes[g, h][:, lo : lo + width].bitcast(FP8X4),
+                        rhs_scale=x_plane[4 * g :, piece * width : (piece + 1) * width],
+                        start=start,
+                        stop=not start,
+                    )
+
+        def evacuate(w, t):
+            results[w, t] = sbuf([P, S], F32, "result%d_%d" % (w, t))
+            width = BANK // 2 if (w, t) == (0, 0) else BANK
+            for piece in range(S // width):
+                nc.scalar.copy(results[w, t][:, piece * width : (piece + 1) * width], accs[w, t, piece][:])
 
         starts = [sum(SLICES[:s]) for s in range(len(SLICES))]
         centres = {}
 
-        def gather_centres(t, tag=None):
-            centres[t] = sbuf([P, V], F32, "centre%d" % t, tag)
-            nc.vector.tensor_copy(centres[t][:], results[0, t][:].indirect(cen_t[:]))
+        def gather_centres(t):
+            centres[t] = sbuf([P, V], F32, "centre%d" % t)[:]
+            nc.vector.tensor_copy(centres[t], results[0, t][:].indirect(cen_t[:]))
 
         first_sums = [sbuf([P, 2, V], F32, "first_sum%d" % d) for d in range(2)]
         last_sums = [sbuf([P, 2, V], F32, "last_sum%d" % d) for d in range(2)]
@@ -166,7 +175,7 @@ def tile_picked_edgecv_gelu_p_kernel(
         }
 
         def add_neighbours(t, d):
-            nc.vector.tensor_tensor((first_sums if t < 2 else last_sums)[d][:, t % 2, :], results[1, t][:].indirect(pos_t[d][:]), centres[t][:], ADD)
+            nc.vector.tensor_tensor((first_sums if t < 2 else last_sums)[d][:, t % 2, :], results[1, t][:].indirect(pos_t[d][:]), centres[t], ADD)
 
         def add_neighbours_of_slice(t, s, d):
             lo, hi = starts[s], starts[s] + SLICES[s]
@@ -212,46 +221,49 @@ def tile_picked_edgecv_gelu_p_kernel(
 
         nc.vector.tensor_copy(x_plane[:], scale_table[:].indirect(offs_t[:]))
         gather_words(0, 0, S)
-        for u in range(2):
-            cast(0, u, u * P // 2)
-            quantise(0, ((2 * u, 2 * u + 1),))
-        gather_words(1, 0, BANK)
-        gather_words(1, BANK, S)
-        for t in range(PACK):
-            multiply(0, t, 0)
-        cast(1, 0, P // 2)
+        cast(0, 0, nc.scalar.copy)
+        quantise(0, ((0, 1),))
+        cast_shared(0, 1, P // 2)
+        quantise(0, ((2, 3),))
+        gather_words(1, 0, S)
+        for t in range(3):
+            multiply(0, t, (0,))
+        cast_shared(1, 0, P // 2)
         quantise(1, ((0,), (1,)))
-        cast(1, 1, 0)
+        cast_shared(1, 1, P // 2)
         quantise(1, ((2, 3),))
-        for t in range(PACK):
-            multiply(0, t, 1)
-        evacuate(0, 0, None, True)
+        for t in range(3):
+            multiply(0, t, (1,))
+        evacuate(0, 0)
+        cast(2, 0, nc.vector.tensor_copy)
+        quantise(2, ((0, 1),))
         gather_centres(0)
         evacuate(0, 1)
         gather_centres(1)
-        cast(2, 0, 0, "w_codes1_1")
-        quantise(2, ((0, 1),))
-        cast(3, 0, P)
+        multiply(0, 3, (0, 1))
+        evacuate(0, 2)
+        cast_shared(3, 0, P // 2)
         quantise(3, ((0, 1),))
+        gather_centres(2)
+        cast(3, 1, nc.scalar.copy)
+        quantise(3, ((2, 3),))
+        evacuate(0, 3)
+        gather_centres(3)
+        for g in range(PASSES):
+            for t in (0, 1):
+                multiply(1, t, (g,))
         for t in (2, 3):
-            evacuate(0, t)
-            gather_centres(t, "w_bf3_0" if t == 2 else None)
-        cast(2, 1, 0, "w_plane1_1")
-        quantise(2, ((2, 3),))
-        for t in (0, 1):
-            for g in range(PASSES):
-                multiply(1, t, g)
+            multiply(1, t, (1,))
         evacuate(1, 0)
         for d in range(2):
             add_neighbours(0, d)
-        cast(3, 1, 0, "w_codes3_0")
-        quantise(3, ((2, 3),))
+        cast(2, 1, nc.scalar.copy, tag="w_codes3_0")
+        quantise(2, ((2, 3),))
         evacuate(1, 1)
         for d in range(2):
             add_neighbours(1, d)
         for t in (2, 3):
-            for g in range(PASSES):
-                multiply(1, t, g)
+            multiply(1, t, (0,))
             evacuate(1, t)
         for d in range(2):
             for s in range(len(SLICES)):

@@ -31,7 +31,7 @@ def tile_picked_edgecv_gelu_p_kernel(
         keep = ctx.enter_context(tc.tile_pool(name="keep", bufs=1))
         psum = ctx.enter_context(tc.psum_pool(name="psum", bufs=1))
         reused = ctx.enter_context(tc.tile_pool(name="reused", bufs=1))
-        places = {"centre2": 0, "w_bf3_0": 1024, "result0_3": 2048}
+        places = {"centre3": 0, "w_bf3_0": 0}
 
         def bank(index, width):
             return psum.tile([P, width], F32, name="bank%d" % index, tag="bank%d" % index)
@@ -170,15 +170,12 @@ def tile_picked_edgecv_gelu_p_kernel(
 
         first_sums = [sbuf([P, 2, V], F32, "first_sum%d" % d) for d in range(2)]
         last_sums = [sbuf([P, 2, V], F32, "last_sum%d" % d) for d in range(2)]
-        acts = {
-            (s, d): sbuf([P, 2, width, 2], BF16, "act%d_%d" % (s, d)) for s, width in enumerate(SLICES) for d in range(2)
-        }
+        acts = [sbuf([P, 2, V, 2], BF16, "act%d" % d) for d in range(2)]
 
         def add_neighbours(t, d):
             nc.vector.tensor_tensor((first_sums if t < 2 else last_sums)[d][:, t % 2, :], results[1, t][:].indirect(pos_t[d][:]), centres[t], ADD)
 
-        def add_neighbours_of_slice(t, s, d):
-            lo, hi = starts[s], starts[s] + SLICES[s]
+        def add_neighbours_between(t, d, lo, hi):
             nc.vector.tensor_tensor(
                 last_sums[d][:, t - 2, lo:hi],
                 results[1, t][:].indirect(pos_t[d][:, lo // 16 : hi // 16]),
@@ -186,18 +183,17 @@ def tile_picked_edgecv_gelu_p_kernel(
                 ADD,
             )
 
-        def activate(u, s, d):
-            lo, hi = starts[s], starts[s] + SLICES[s]
+        def activate(u, d, lo, hi):
             source = (first_sums if u == 0 else last_sums)[d][:, :, lo:hi]
-            nc.scalar.activation(acts[s, d][:, u], source.rearrange("p e v -> p v e"), GELU, bias=zero_bias[:])
+            nc.scalar.activation(acts[d][:, u, lo:hi], source.rearrange("p e v -> p v e"), GELU, bias=zero_bias[:])
 
         def project(s):
             width = SLICES[s]
             z_bf = sbuf([P, width, 2, 2], BF16, "z_bf%d" % s)
             nc.vector.tensor_tensor(
                 z_bf[:],
-                acts[s, 0][:].rearrange("p u v e -> p v u e"),
-                acts[s, 1][:].rearrange("p u v e -> p v u e"),
+                acts[0][:, :, starts[s] : starts[s] + width].rearrange("p u v e -> p v u e"),
+                acts[1][:, :, starts[s] : starts[s] + width].rearrange("p u v e -> p v u e"),
                 MAX,
             )
             z_codes = sbuf([P, width], U32, "z_codes%d" % s)
@@ -242,13 +238,14 @@ def tile_picked_edgecv_gelu_p_kernel(
         gather_centres(1)
         multiply(0, 3, (0, 1))
         evacuate(0, 2)
-        cast_shared(3, 0, P // 2)
-        quantise(3, ((0, 1),))
         gather_centres(2)
+        evacuate(0, 3)
+        w_bf[3, 0] = sbuf([P, 2, P, PACK], BF16, "w_bf3_0")
+        nc.gpsimd.tensor_copy(w_bf[3, 0][:], raw[3][:].rearrange("p j (m u e) -> p u e m j", u=2, e=2)[:, 0])
+        quantise(3, ((0, 1),))
+        gather_centres(3)
         cast(3, 1, nc.scalar.copy)
         quantise(3, ((2, 3),))
-        evacuate(0, 3)
-        gather_centres(3)
         for g in range(PASSES):
             for t in (0, 1):
                 multiply(1, t, (g,))
@@ -266,15 +263,16 @@ def tile_picked_edgecv_gelu_p_kernel(
             multiply(1, t, (0,))
             evacuate(1, t)
         for d in range(2):
-            for s in range(len(SLICES)):
-                activate(0, s, d)
+            activate(0, d, 0, V)
         for d in range(2):
             add_neighbours(2, d)
-        for s in range(len(SLICES)):
+        for lo in (0, V // 2):
             for d in range(2):
-                add_neighbours_of_slice(3, s, d)
-        for s in range(len(SLICES)):
-            for d in range(2):
-                activate(1, s, d)
+                add_neighbours_between(3, d, lo, lo + V // 2)
+        for d in range(2):
+            activate(1, d, 0, V // 2)
+        activate(1, 0, V // 2, V)
+        for s in (1, 2):
+            activate(1, 1, starts[s], starts[s] + SLICES[s])
         for s in range(len(SLICES)):
             project(s)

@@ -51,7 +51,6 @@ def tile_picked_edgecv_gelu_p_kernel(
         scale_table = sbuf([P, T], U8, "scale_table")
         nc.vector.memset(scale_table[:, : T // 2].bitcast(I32), 0)
         nc.gpsimd.memset(scale_table[:, T // 2 :].bitcast(I32), 0)
-        offs_t = load_list(offs, "offs_t")
         word_tables = [sbuf([P, T], I32, "word_table%d" % g) for g in range(PASSES)]
 
         def load_words(g, lo, hi):
@@ -59,6 +58,7 @@ def tile_picked_edgecv_gelu_p_kernel(
             nc.sync.dma_start(word_tables[g][:, lo:hi], words[:, lo:hi])
 
         load_words(0, 0, 3 * T // 8)
+        offs_t = load_list(offs, "offs_t")
         for q in range(4):
             nc.sync.dma_start(
                 scale_table[32 * q : 32 * q + 4 * PASSES, :].bitcast(I32),
@@ -73,17 +73,19 @@ def tile_picked_edgecv_gelu_p_kernel(
 
         raw = {}
 
-        def load_weights(r):
+        def load_weights(r, pieces=1):
             w, g = rounds[r]
             raw[r] = sbuf([P, PACK, H], F32, "raw%d" % r)
-            rows = w[g * P * PACK : (g + 1) * P * PACK, :]
-            nc.sync.dma_start(raw[r][:], rows.rearrange("(p j) c -> p j c", j=PACK))
+            rows = w[g * P * PACK : (g + 1) * P * PACK, :].rearrange("(p j) c -> p j c", j=PACK)
+            step = PACK // pieces
+            for j in range(0, PACK, step):
+                nc.sync.dma_start(raw[r][:, j : j + step], rows[:, j : j + step])
 
         load_words(0, 3 * T // 8, T)
         load_weights(0)
         load_words(1, 0, T)
         load_weights(1)
-        load_weights(2)
+        load_weights(2, 2)
         cen_t = load_list(cen, "cen_t")
         load_weights(3)
         pos_t = [load_list(pos1, "pos1_t"), load_list(pos2, "pos2_t")]
@@ -108,12 +110,18 @@ def tile_picked_edgecv_gelu_p_kernel(
         w_codes = {}
         w_plane = {}
 
-        def cast(r, u, copy, lo=0, hi=P, tag=None):
+        def cast(r, u, copy, lo=0, hi=P, tag=None, rows=slice(0, PACK)):
             if (r, u) not in w_bf:
                 w_bf[r, u] = sbuf([P, 2, P, PACK], BF16, "w_bf%d_%d" % (r, u), tag)
             src = raw[r][:].rearrange("p j (m u e) -> p u m j e", u=2, e=2)[:, u]
             dst = w_bf[r, u][:].rearrange("p e m j -> p m j e")
-            copy(dst[:, lo:hi], src[:, lo:hi])
+            copy(dst[:, lo:hi, rows], src[:, lo:hi, rows])
+
+        def cast_on_gpsimd(r, u, lo, hi):
+            if (r, u) not in w_bf:
+                w_bf[r, u] = sbuf([P, 2, P, PACK], BF16, "w_bf%d_%d" % (r, u))
+            src = raw[r][:].rearrange("p j (m u e) -> p u e m j", u=2, e=2)[:, u]
+            nc.gpsimd.tensor_copy(w_bf[r, u][:, :, lo:hi], src[:, :, lo:hi])
 
         def cast_shared(r, u, on_vector):
             cast(r, u, nc.vector.tensor_copy, 0, on_vector)
@@ -135,10 +143,10 @@ def tile_picked_edgecv_gelu_p_kernel(
         accs = {}
         results = {}
 
-        first_bank = {(0, 0): 0, (0, 1): 4, (0, 2): 6, (0, 3): 0, (1, 0): 2, (1, 1): 4, (1, 2): 6, (1, 3): 0}
+        first_bank = {(0, 0): 0, (0, 1): 4, (0, 2): 6, (0, 3): 0, (1, 0): 2, (1, 1): 6, (1, 2): 0, (1, 3): 2}
 
         def multiply(w, t, passes):
-            width = BANK // 2 if (w, t) == (0, 0) else BANK
+            width = BANK // 2 if t == 0 else BANK
             for piece in range(S // width):
                 h, lo = divmod(piece * width, BANK)
                 for g in passes:
@@ -157,7 +165,7 @@ def tile_picked_edgecv_gelu_p_kernel(
 
         def evacuate(w, t):
             results[w, t] = sbuf([P, S], F32, "result%d_%d" % (w, t))
-            width = BANK // 2 if (w, t) == (0, 0) else BANK
+            width = BANK // 2 if t == 0 else BANK
             for piece in range(S // width):
                 nc.scalar.copy(results[w, t][:, piece * width : (piece + 1) * width], accs[w, t, piece][:])
 
@@ -201,7 +209,7 @@ def tile_picked_edgecv_gelu_p_kernel(
             nc.vector.quantize_mx(
                 out=z_codes[:].bitcast(FP8X4), scales=z_plane[:], in_=z_bf[:].rearrange("p v u e -> p (v u e)")
             )
-            acc = bank(s, width)
+            acc = bank(4 + s, width)
             nc.tensor.matmul_mx(
                 out=acc[:],
                 lhsT=w3_codes[:].bitcast(FP8X4),
@@ -219,7 +227,8 @@ def tile_picked_edgecv_gelu_p_kernel(
         gather_words(0, 0, S)
         cast(0, 0, nc.scalar.copy)
         quantise(0, ((0, 1),))
-        cast_shared(0, 1, P // 2)
+        cast_on_gpsimd(0, 1, 0, P // 2)
+        cast(0, 1, nc.scalar.copy, P // 2, P)
         quantise(0, ((2, 3),))
         gather_words(1, 0, S)
         for t in range(3):
@@ -231,7 +240,8 @@ def tile_picked_edgecv_gelu_p_kernel(
         for t in range(3):
             multiply(0, t, (1,))
         evacuate(0, 0)
-        cast(2, 0, nc.vector.tensor_copy)
+        for j in (0, 2):
+            cast(2, 0, nc.vector.tensor_copy, rows=slice(j, j + 2))
         quantise(2, ((0, 1),))
         gather_centres(0)
         evacuate(0, 1)
@@ -240,8 +250,7 @@ def tile_picked_edgecv_gelu_p_kernel(
         evacuate(0, 2)
         gather_centres(2)
         evacuate(0, 3)
-        w_bf[3, 0] = sbuf([P, 2, P, PACK], BF16, "w_bf3_0")
-        nc.gpsimd.tensor_copy(w_bf[3, 0][:], raw[3][:].rearrange("p j (m u e) -> p u e m j", u=2, e=2)[:, 0])
+        cast_on_gpsimd(3, 0, 0, P)
         quantise(3, ((0, 1),))
         gather_centres(3)
         cast(3, 1, nc.scalar.copy)

@@ -227,8 +227,8 @@ def tile_picked_edgecv_gelu_p_kernel(
         gather_words(0, 0, S)
         cast(0, 0, nc.scalar.copy)
         quantise(0, ((0, 1),))
-        cast_on_gpsimd(0, 1, 0, P // 2)
-        cast(0, 1, nc.scalar.copy, P // 2, P)
+        cast_on_gpsimd(0, 1, 0, 5 * P // 8)
+        cast(0, 1, nc.scalar.copy, 5 * P // 8, P)
         quantise(0, ((2, 3),))
         gather_words(1, 0, S)
         for t in range(3):
@@ -250,11 +250,12 @@ def tile_picked_edgecv_gelu_p_kernel(
         evacuate(0, 2)
         gather_centres(2)
         evacuate(0, 3)
-        cast_on_gpsimd(3, 0, 0, P)
-        quantise(3, ((0, 1),))
+        cast_on_gpsimd(3, 0, 0, 7 * P // 8)
+        cast(3, 0, nc.scalar.copy, 7 * P // 8, P)
+        quantise(3, ((0,), (1,)))
         gather_centres(3)
         cast(3, 1, nc.scalar.copy)
-        quantise(3, ((2, 3),))
+        quantise(3, ((2, 3),), "result0_3")
         for g in range(PASSES):
             for t in (0, 1):
                 multiply(1, t, (g,))

@@ -19,8 +19,18 @@ MAX = mybir.AluOpType.max
 P = 128
 PACK = 4
 PASSES = K // (P * PACK)
+QUADRANT = 32
+PLANE_ROWS = 4
+LIST_ROWS = 16
 BANK = 512
+Y, E = 0, 1
+
+EARLY_COLUMNS = 3 * T // 8
+GPSIMD_SHARE_PART_0 = 5 * P // 8
+GPSIMD_SHARE_PART_3 = 3 * P // 4
 SLICES = (256, 128, 128)
+FIRST_BANK = {(Y, 0): 0, (Y, 1): 4, (Y, 2): 6, (Y, 3): 0, (E, 0): 2, (E, 1): 6, (E, 2): 0, (E, 3): 2}
+FIRST_OUT_BANK = 4
 
 
 def tile_picked_edgecv_gelu_p_kernel(
@@ -31,14 +41,13 @@ def tile_picked_edgecv_gelu_p_kernel(
         keep = ctx.enter_context(tc.tile_pool(name="keep", bufs=1))
         psum = ctx.enter_context(tc.psum_pool(name="psum", bufs=1))
         reused = ctx.enter_context(tc.tile_pool(name="reused", bufs=1))
-        places = {"centre3": 0, "w_bf3_0": 0}
 
         def bank(index, width):
             return psum.tile([P, width], F32, name="bank%d" % index, tag="bank%d" % index)
 
         def sbuf(shape, dtype, name, tag=None):
-            if name in places:
-                return reused.tile(shape, dtype, name=name, tag=name, align_bytes=64, offset=places[name])
+            if name in ("w_bf3_0", "centre3"):
+                return reused.tile(shape, dtype, name=name, tag=name, align_bytes=64, offset=0)
             return keep.tile(shape, dtype, name=name, tag=tag or name, align_bytes=64)
 
         def load_list(source, name):
@@ -46,7 +55,6 @@ def tile_picked_edgecv_gelu_p_kernel(
             nc.sync.dma_start(tile[:], source)
             return tile
 
-        rounds = [(w, g) for w in (w1, w2) for g in range(PASSES)]
 
         scale_table = sbuf([P, T], U8, "scale_table")
         nc.vector.memset(scale_table[:, : T // 2].bitcast(I32), 0)
@@ -57,12 +65,12 @@ def tile_picked_edgecv_gelu_p_kernel(
             words = x_words[g].rearrange("p n t -> p (n t)").bitcast(I32)
             nc.sync.dma_start(word_tables[g][:, lo:hi], words[:, lo:hi])
 
-        load_words(0, 0, 3 * T // 8)
+        load_words(0, 0, EARLY_COLUMNS)
         offs_t = load_list(offs, "offs_t")
-        for q in range(4):
+        for q in range(P // QUADRANT):
             nc.sync.dma_start(
-                scale_table[32 * q : 32 * q + 4 * PASSES, :].bitcast(I32),
-                x_scales[:, 4 * q : 4 * q + 4, :].bitcast(I32),
+                scale_table[QUADRANT * q : QUADRANT * q + PLANE_ROWS * PASSES, :].bitcast(I32),
+                x_scales[:, PLANE_ROWS * q : PLANE_ROWS * (q + 1), :].bitcast(I32),
             )
         zero_in = keep.tile([P, 1], F32, name="zero_in")
         nc.vector.memset(zero_in[:], 0.0)
@@ -72,136 +80,132 @@ def tile_picked_edgecv_gelu_p_kernel(
         nc.vector.memset(w3_plane[:].bitcast(I32), 0)
 
         raw = {}
+        all_rows = slice(0, PACK)
+        row_halves = (slice(0, PACK // 2), slice(PACK // 2, PACK))
 
-        def load_weights(r, pieces=1):
-            w, g = rounds[r]
-            raw[r] = sbuf([P, PACK, H], F32, "raw%d" % r)
-            rows = w[g * P * PACK : (g + 1) * P * PACK, :].rearrange("(p j) c -> p j c", j=PACK)
-            step = PACK // pieces
-            for j in range(0, PACK, step):
-                nc.sync.dma_start(raw[r][:, j : j + step], rows[:, j : j + step])
+        def load_part(part, pieces=(all_rows,)):
+            w, g = (w1, w2)[part // PASSES], part % PASSES
+            raw[part] = sbuf([P, PACK, H], F32, "raw%d" % part)
+            source = w[g * P * PACK : (g + 1) * P * PACK, :].rearrange("(p j) c -> p j c", j=PACK)
+            for rows in pieces:
+                nc.sync.dma_start(raw[part][:, rows], source[:, rows])
 
-        load_words(0, 3 * T // 8, T)
-        load_weights(0)
+        load_words(0, EARLY_COLUMNS, T)
+        load_part(0)
         load_words(1, 0, T)
-        load_weights(1)
-        load_weights(2, 2)
+        load_part(1)
+        load_part(2, row_halves)
         cen_t = load_list(cen, "cen_t")
-        load_weights(3)
+        load_part(3)
         pos_t = [load_list(pos1, "pos1_t"), load_list(pos2, "pos2_t")]
         w3_codes = sbuf([P, N], I32, "w3_codes")
         nc.sync.dma_start(w3_codes[:], w3_words[0].rearrange("p n t -> p (n t)").bitcast(I32))
-        for q in range(4):
+        for q in range(P // QUADRANT):
             nc.sync.dma_start(
-                w3_plane[32 * q : 32 * q + 4, :].bitcast(I32),
-                w3_scales[0, 4 * q : 4 * q + 4, :].bitcast(I32),
+                w3_plane[QUADRANT * q : QUADRANT * q + PLANE_ROWS, :].bitcast(I32),
+                w3_scales[0, PLANE_ROWS * q : PLANE_ROWS * (q + 1), :].bitcast(I32),
             )
+
 
         x_plane = sbuf([P, S], U8, "x_plane")
         x_codes = {}
 
-        def gather_words(g, lo, hi):
-            tile = sbuf([P, hi - lo], U32, "x_codes%d_%d" % (g, lo))
-            nc.vector.tensor_copy(tile[:], word_tables[g][:].bitcast(U32).indirect(offs_t[:, lo // 16 : hi // 16]))
-            for h in range(lo // BANK, hi // BANK):
-                x_codes[g, h] = tile[:, h * BANK - lo : (h + 1) * BANK - lo]
+        def gather_words(g):
+            x_codes[g] = sbuf([P, S], U32, "x_codes%d_0" % g)
+            nc.vector.tensor_copy(x_codes[g][:], word_tables[g][:].bitcast(U32).indirect(offs_t[:]))
 
         w_bf = {}
         w_codes = {}
         w_plane = {}
 
-        def cast(r, u, copy, lo=0, hi=P, tag=None, rows=slice(0, PACK)):
-            if (r, u) not in w_bf:
-                w_bf[r, u] = sbuf([P, 2, P, PACK], BF16, "w_bf%d_%d" % (r, u), tag)
-            src = raw[r][:].rearrange("p j (m u e) -> p u m j e", u=2, e=2)[:, u]
-            dst = w_bf[r, u][:].rearrange("p e m j -> p m j e")
-            copy(dst[:, lo:hi, rows], src[:, lo:hi, rows])
+        def rounded_pair(part, u, tag=None):
+            if (part, u) not in w_bf:
+                w_bf[part, u] = sbuf([P, 2, P, PACK], BF16, "w_bf%d_%d" % (part, u), tag)
+            return w_bf[part, u]
 
-        def cast_on_gpsimd(r, u, lo, hi):
-            if (r, u) not in w_bf:
-                w_bf[r, u] = sbuf([P, 2, P, PACK], BF16, "w_bf%d_%d" % (r, u))
-            src = raw[r][:].rearrange("p j (m u e) -> p u e m j", u=2, e=2)[:, u]
-            nc.gpsimd.tensor_copy(w_bf[r, u][:, :, lo:hi], src[:, :, lo:hi])
+        def round_pair(part, u, copy, lo=0, hi=P, tag=None, rows=all_rows):
+            source = raw[part][:].rearrange("p j (m u e) -> p u m j e", u=2, e=2)[:, u]
+            target = rounded_pair(part, u, tag)[:].rearrange("p e m j -> p m j e")
+            copy(target[:, lo:hi, rows], source[:, lo:hi, rows])
 
-        def cast_shared(r, u, on_vector):
-            cast(r, u, nc.vector.tensor_copy, 0, on_vector)
-            cast(r, u, nc.scalar.copy, on_vector, P)
+        def round_with_gpsimd(part, u, share):
+            source = raw[part][:].rearrange("p j (m u e) -> p u e m j", u=2, e=2)[:, u]
+            nc.gpsimd.tensor_copy(rounded_pair(part, u)[:, :, :share], source[:, :, :share])
+            round_pair(part, u, nc.scalar.copy, share, P)
 
-        def quantise(r, groups, tag=None):
-            for ts in groups:
-                codes = sbuf([P, len(ts) * P], U32, "w_codes%d_%d" % (r, ts[0]), tag)
-                plane = sbuf([P, len(ts) * P], U8, "w_plane%d_%d" % (r, ts[0]))
-                nc.vector.quantize_mx(
-                    out=codes[:].bitcast(FP8X4),
-                    scales=plane[:],
-                    in_=w_bf[r, ts[0] // 2][:, ts[0] % 2 : ts[-1] % 2 + 1].rearrange("p t m j -> p (t m j)"),
-                )
-                for a, t in enumerate(ts):
-                    w_codes[r, t] = codes[:, a * P : (a + 1) * P]
-                    w_plane[r, t] = plane[:, a * P : (a + 1) * P]
+        def round_with_vector(part, u):
+            round_pair(part, u, nc.vector.tensor_copy, 0, P // 2)
+            round_pair(part, u, nc.scalar.copy, P // 2, P)
+
+        def quantise(part, hands, tag=None):
+            first = hands[0]
+            codes = sbuf([P, len(hands) * P], U32, "w_codes%d_%d" % (part, first), tag)
+            plane = sbuf([P, len(hands) * P], U8, "w_plane%d_%d" % (part, first))
+            values = w_bf[part, first // 2][:, first % 2 : first % 2 + len(hands)]
+            nc.vector.quantize_mx(
+                out=codes[:].bitcast(FP8X4), scales=plane[:], in_=values.rearrange("p e m j -> p (e m j)")
+            )
+            for place, t in enumerate(hands):
+                w_codes[part, t] = codes[:, place * P : (place + 1) * P]
+                w_plane[part, t] = plane[:, place * P : (place + 1) * P]
 
         accs = {}
         results = {}
 
-        first_bank = {(0, 0): 0, (0, 1): 4, (0, 2): 6, (0, 3): 0, (1, 0): 2, (1, 1): 6, (1, 2): 0, (1, 3): 2}
-
-        def multiply(w, t, passes):
+        def pieces_of(t):
             width = BANK // 2 if t == 0 else BANK
-            for piece in range(S // width):
-                h, lo = divmod(piece * width, BANK)
+            return [slice(lo, lo + width) for lo in range(0, S, width)]
+
+        def multiply(result, t, passes):
+            for piece, columns in enumerate(pieces_of(t)):
                 for g in passes:
-                    start = (w, t, piece) not in accs
+                    start = (result, t, piece) not in accs
                     if start:
-                        accs[w, t, piece] = bank(first_bank[w, t] + piece, width)
+                        accs[result, t, piece] = bank(FIRST_BANK[result, t] + piece, columns.stop - columns.start)
                     nc.tensor.matmul_mx(
-                        out=accs[w, t, piece][:],
-                        lhsT=w_codes[PASSES * w + g, t].bitcast(FP8X4),
-                        lhsT_scale=w_plane[PASSES * w + g, t],
-                        rhs=x_codes[g, h][:, lo : lo + width].bitcast(FP8X4),
-                        rhs_scale=x_plane[4 * g :, piece * width : (piece + 1) * width],
+                        out=accs[result, t, piece][:],
+                        lhsT=w_codes[PASSES * result + g, t].bitcast(FP8X4),
+                        lhsT_scale=w_plane[PASSES * result + g, t],
+                        rhs=x_codes[g][:, columns].bitcast(FP8X4),
+                        rhs_scale=x_plane[PLANE_ROWS * g :, columns],
                         start=start,
                         stop=not start,
                     )
 
-        def evacuate(w, t):
-            results[w, t] = sbuf([P, S], F32, "result%d_%d" % (w, t))
-            width = BANK // 2 if t == 0 else BANK
-            for piece in range(S // width):
-                nc.scalar.copy(results[w, t][:, piece * width : (piece + 1) * width], accs[w, t, piece][:])
+        def evacuate(result, t, first_copy=nc.scalar.copy):
+            results[result, t] = sbuf([P, S], F32, "result%d_%d" % (result, t))
+            for piece, columns in enumerate(pieces_of(t)):
+                copy = first_copy if piece == 0 else nc.scalar.copy
+                copy(results[result, t][:, columns], accs[result, t, piece][:])
 
-        starts = [sum(SLICES[:s]) for s in range(len(SLICES))]
         centres = {}
 
         def gather_centres(t):
-            centres[t] = sbuf([P, V], F32, "centre%d" % t)[:]
-            nc.vector.tensor_copy(centres[t], results[0, t][:].indirect(cen_t[:]))
+            centres[t] = sbuf([P, V], F32, "centre%d" % t)
+            nc.vector.tensor_copy(centres[t][:], results[Y, t][:].indirect(cen_t[:]))
 
-        first_sums = [sbuf([P, 2, V], F32, "first_sum%d" % d) for d in range(2)]
-        last_sums = [sbuf([P, 2, V], F32, "last_sum%d" % d) for d in range(2)]
+        sums = [[sbuf([P, 2, V], F32, "%s_sum%d" % (name, d)) for d in range(2)] for name in ("first", "last")]
         acts = [sbuf([P, 2, V, 2], BF16, "act%d" % d) for d in range(2)]
 
-        def add_neighbours(t, d):
-            nc.vector.tensor_tensor((first_sums if t < 2 else last_sums)[d][:, t % 2, :], results[1, t][:].indirect(pos_t[d][:]), centres[t], ADD)
-
-        def add_neighbours_between(t, d, lo, hi):
+        def add_neighbours(t, d, lo=0, hi=V):
             nc.vector.tensor_tensor(
-                last_sums[d][:, t - 2, lo:hi],
-                results[1, t][:].indirect(pos_t[d][:, lo // 16 : hi // 16]),
+                sums[t // 2][d][:, t % 2, lo:hi],
+                results[E, t][:].indirect(pos_t[d][:, lo // LIST_ROWS : hi // LIST_ROWS]),
                 centres[t][:, lo:hi],
                 ADD,
             )
 
         def activate(u, d, lo, hi):
-            source = (first_sums if u == 0 else last_sums)[d][:, :, lo:hi]
-            nc.scalar.activation(acts[d][:, u, lo:hi], source.rearrange("p e v -> p v e"), GELU, bias=zero_bias[:])
+            source = sums[u][d][:, :, lo:hi].rearrange("p e v -> p v e")
+            nc.scalar.activation(acts[d][:, u, lo:hi], source, GELU, bias=zero_bias[:])
 
-        def project(s):
-            width = SLICES[s]
+        def project(s, lo, hi):
+            width = hi - lo
             z_bf = sbuf([P, width, 2, 2], BF16, "z_bf%d" % s)
             nc.vector.tensor_tensor(
                 z_bf[:],
-                acts[0][:, :, starts[s] : starts[s] + width].rearrange("p u v e -> p v u e"),
-                acts[1][:, :, starts[s] : starts[s] + width].rearrange("p u v e -> p v u e"),
+                acts[0][:, :, lo:hi].rearrange("p u v e -> p v u e"),
+                acts[1][:, :, lo:hi].rearrange("p u v e -> p v u e"),
                 MAX,
             )
             z_codes = sbuf([P, width], U32, "z_codes%d" % s)
@@ -209,7 +213,7 @@ def tile_picked_edgecv_gelu_p_kernel(
             nc.vector.quantize_mx(
                 out=z_codes[:].bitcast(FP8X4), scales=z_plane[:], in_=z_bf[:].rearrange("p v u e -> p (v u e)")
             )
-            acc = bank(4 + s, width)
+            acc = bank(FIRST_OUT_BANK + s, width)
             nc.tensor.matmul_mx(
                 out=acc[:],
                 lhsT=w3_codes[:].bitcast(FP8X4),
@@ -221,68 +225,77 @@ def tile_picked_edgecv_gelu_p_kernel(
             )
             staged = sbuf([P, width], F32, "staged%d" % s)
             nc.scalar.copy(staged[:], acc[:])
-            nc.sync.dma_start(out[:, starts[s] : starts[s] + width], staged[:])
+            nc.sync.dma_start(out[:, lo:hi], staged[:])
+
 
         nc.vector.tensor_copy(x_plane[:], scale_table[:].indirect(offs_t[:]))
-        gather_words(0, 0, S)
-        cast(0, 0, nc.scalar.copy)
-        quantise(0, ((0, 1),))
-        cast_on_gpsimd(0, 1, 0, 5 * P // 8)
-        cast(0, 1, nc.scalar.copy, 5 * P // 8, P)
-        quantise(0, ((2, 3),))
-        gather_words(1, 0, S)
+        gather_words(0)
+        round_pair(0, 0, nc.scalar.copy)
+        quantise(0, (0, 1))
+        round_with_gpsimd(0, 1, GPSIMD_SHARE_PART_0)
+        quantise(0, (2, 3))
+        gather_words(1)
         for t in range(3):
-            multiply(0, t, (0,))
-        cast_shared(1, 0, P // 2)
-        quantise(1, ((0,), (1,)))
-        cast_shared(1, 1, P // 2)
-        quantise(1, ((2, 3),))
+            multiply(Y, t, (0,))
+        round_with_vector(1, 0)
+        quantise(1, (0,))
+        quantise(1, (1,))
+        round_with_vector(1, 1)
+        quantise(1, (2, 3))
         for t in range(3):
-            multiply(0, t, (1,))
-        evacuate(0, 0)
-        for j in (0, 2):
-            cast(2, 0, nc.vector.tensor_copy, rows=slice(j, j + 2))
-        quantise(2, ((0, 1),))
+            multiply(Y, t, (1,))
+        evacuate(Y, 0)
+
+
+        for rows in row_halves:
+            round_pair(2, 0, nc.vector.tensor_copy, rows=rows)
+        quantise(2, (0, 1))
         gather_centres(0)
-        evacuate(0, 1)
+        evacuate(Y, 1)
         gather_centres(1)
-        multiply(0, 3, (0, 1))
-        evacuate(0, 2)
+        multiply(Y, 3, (0, 1))
+        evacuate(Y, 2)
         gather_centres(2)
-        evacuate(0, 3)
-        cast_on_gpsimd(3, 0, 0, 7 * P // 8)
-        cast(3, 0, nc.scalar.copy, 7 * P // 8, P)
-        quantise(3, ((0,), (1,)))
+        evacuate(Y, 3)
+        round_with_gpsimd(3, 0, GPSIMD_SHARE_PART_3)
+        quantise(3, (0,))
+        quantise(3, (1,))
         gather_centres(3)
-        cast(3, 1, nc.scalar.copy)
-        quantise(3, ((2, 3),), "result0_3")
+        round_pair(3, 1, nc.scalar.copy)
+        quantise(3, (2, 3), "result0_3")
+
+
         for g in range(PASSES):
             for t in (0, 1):
-                multiply(1, t, (g,))
+                multiply(E, t, (g,))
         for t in (2, 3):
-            multiply(1, t, (1,))
-        evacuate(1, 0)
+            multiply(E, t, (1,))
+        evacuate(E, 0, nc.vector.tensor_copy)
         for d in range(2):
             add_neighbours(0, d)
-        cast(2, 1, nc.scalar.copy, tag="w_codes3_0")
-        quantise(2, ((2, 3),))
-        evacuate(1, 1)
+        round_pair(2, 1, nc.scalar.copy, tag="w_codes3_0")
+        quantise(2, (2, 3))
+        evacuate(E, 1)
         for d in range(2):
             add_neighbours(1, d)
         for t in (2, 3):
-            multiply(1, t, (0,))
-            evacuate(1, t)
+            multiply(E, t, (0,))
+            evacuate(E, t)
         for d in range(2):
             activate(0, d, 0, V)
         for d in range(2):
             add_neighbours(2, d)
-        for lo in (0, V // 2):
+
+
+        half = V // 2
+        for lo in (0, half):
             for d in range(2):
-                add_neighbours_between(3, d, lo, lo + V // 2)
+                add_neighbours(3, d, lo, lo + half)
         for d in range(2):
-            activate(1, d, 0, V // 2)
-        activate(1, 0, V // 2, V)
-        for s in (1, 2):
-            activate(1, 1, starts[s], starts[s] + SLICES[s])
-        for s in range(len(SLICES)):
-            project(s)
+            activate(1, d, 0, half)
+        activate(1, 0, half, V)
+        bounds = [(sum(SLICES[:s]), sum(SLICES[: s + 1])) for s in range(len(SLICES))]
+        for lo, hi in bounds[1:]:
+            activate(1, 1, lo, hi)
+        for s, (lo, hi) in enumerate(bounds):
+            project(s, lo, hi)

@@ -13,6 +13,7 @@ U16 = mybir.dt.uint16
 U8 = mybir.dt.uint8
 FP8X4 = mybir.dt.float8_e4m3fn_x4
 GELU = mybir.ActivationFunctionType.Gelu_apprx_tanh
+COPY = mybir.ActivationFunctionType.Copy
 ADD = mybir.AluOpType.add
 MAX = mybir.AluOpType.max
 
@@ -27,10 +28,9 @@ Y, E = 0, 1
 
 EARLY_COLUMNS = 3 * T // 8
 GPSIMD_SHARE_PART_0 = 5 * P // 8
-GPSIMD_SHARE_PART_3 = 3 * P // 4
 SLICES = (256, 128, 128)
-FIRST_BANK = {(Y, 0): 0, (Y, 1): 4, (Y, 2): 6, (Y, 3): 0, (E, 0): 2, (E, 1): 6, (E, 2): 0, (E, 3): 2}
-FIRST_OUT_BANK = 4
+FIRST_BANK = {(Y, 0): 0, (Y, 1): 4, (Y, 2): 6, (Y, 3): 0, (E, 0): 2, (E, 1): 6, (E, 2): 2, (E, 3): 4}
+OUT_BANKS = (6, 7, 0)
 
 
 def tile_picked_edgecv_gelu_p_kernel(
@@ -40,14 +40,11 @@ def tile_picked_edgecv_gelu_p_kernel(
     with ExitStack() as ctx:
         keep = ctx.enter_context(tc.tile_pool(name="keep", bufs=1))
         psum = ctx.enter_context(tc.psum_pool(name="psum", bufs=1))
-        reused = ctx.enter_context(tc.tile_pool(name="reused", bufs=1))
 
         def bank(index, width):
             return psum.tile([P, width], F32, name="bank%d" % index, tag="bank%d" % index)
 
         def sbuf(shape, dtype, name, tag=None):
-            if name in ("w_bf3_0", "centre3"):
-                return reused.tile(shape, dtype, name=name, tag=name, align_bytes=64, offset=0)
             return keep.tile(shape, dtype, name=name, tag=tag or name, align_bytes=64)
 
         def load_list(source, name):
@@ -118,32 +115,31 @@ def tile_picked_edgecv_gelu_p_kernel(
         w_codes = {}
         w_plane = {}
 
-        def rounded_pair(part, u, tag=None):
-            if (part, u) not in w_bf:
-                w_bf[part, u] = sbuf([P, 2, P, PACK], BF16, "w_bf%d_%d" % (part, u), tag)
-            return w_bf[part, u]
+        def rounded(part, hands, tag=None):
+            if (part, hands.start) not in w_bf:
+                shape = [P, len(hands), P, PACK]
+                w_bf[part, hands.start] = sbuf(shape, BF16, "w_bf%d_%d" % (part, hands.start), tag)
+            return w_bf[part, hands.start]
 
-        def round_pair(part, u, copy, lo=0, hi=P, tag=None, rows=all_rows):
-            source = raw[part][:].rearrange("p j (m u e) -> p u m j e", u=2, e=2)[:, u]
-            target = rounded_pair(part, u, tag)[:].rearrange("p e m j -> p m j e")
+        def round_hands(part, hands, copy, lo=0, hi=P, rows=all_rows):
+            source = raw[part][:].rearrange("p j (m t) -> p m j t", t=PACK)[:, :, :, hands.start : hands.stop]
+            target = rounded(part, hands)[:].rearrange("p t m j -> p m j t")
             copy(target[:, lo:hi, rows], source[:, lo:hi, rows])
 
-        def round_with_gpsimd(part, u, share):
-            source = raw[part][:].rearrange("p j (m u e) -> p u e m j", u=2, e=2)[:, u]
-            nc.gpsimd.tensor_copy(rounded_pair(part, u)[:, :, :share], source[:, :, :share])
-            round_pair(part, u, nc.scalar.copy, share, P)
+        def round_on_gpsimd(part, hands, share=P, tag=None):
+            source = raw[part][:].rearrange("p j (m t) -> p t m j", t=PACK)[:, hands.start : hands.stop]
+            nc.gpsimd.tensor_copy(rounded(part, hands, tag)[:, :, :share], source[:, :, :share])
 
-        def round_with_vector(part, u):
-            round_pair(part, u, nc.vector.tensor_copy, 0, P // 2)
-            round_pair(part, u, nc.scalar.copy, P // 2, P)
+        def round_with_vector(part, hands):
+            round_hands(part, hands, nc.vector.tensor_copy, 0, P // 2)
+            round_hands(part, hands, nc.scalar.copy, P // 2, P)
 
-        def quantise(part, hands, tag=None):
-            first = hands[0]
-            codes = sbuf([P, len(hands) * P], U32, "w_codes%d_%d" % (part, first), tag)
-            plane = sbuf([P, len(hands) * P], U8, "w_plane%d_%d" % (part, first))
-            values = w_bf[part, first // 2][:, first % 2 : first % 2 + len(hands)]
+        def quantise(part, tile_start, hands, tag=None):
+            codes = sbuf([P, len(hands) * P], U32, "w_codes%d_%d" % (part, hands.start), tag)
+            plane = sbuf([P, len(hands) * P], U8, "w_plane%d_%d" % (part, hands.start))
+            values = w_bf[part, tile_start][:, hands.start - tile_start : hands.stop - tile_start]
             nc.vector.quantize_mx(
-                out=codes[:].bitcast(FP8X4), scales=plane[:], in_=values.rearrange("p e m j -> p (e m j)")
+                out=codes[:].bitcast(FP8X4), scales=plane[:], in_=values.rearrange("p t m j -> p (t m j)")
             )
             for place, t in enumerate(hands):
                 w_codes[part, t] = codes[:, place * P : (place + 1) * P]
@@ -172,17 +168,21 @@ def tile_picked_edgecv_gelu_p_kernel(
                         stop=not start,
                     )
 
-        def evacuate(result, t, first_copy=nc.scalar.copy):
-            results[result, t] = sbuf([P, S], F32, "result%d_%d" % (result, t))
+        def evacuate(result, t, first_copy=nc.scalar.copy, tag=None):
+            results[result, t] = sbuf([P, S], F32, "result%d_%d" % (result, t), tag)
             for piece, columns in enumerate(pieces_of(t)):
                 copy = first_copy if piece == 0 else nc.scalar.copy
                 copy(results[result, t][:, columns], accs[result, t, piece][:])
 
         centres = {}
 
-        def gather_centres(t):
-            centres[t] = sbuf([P, V], F32, "centre%d" % t)
-            nc.vector.tensor_copy(centres[t][:], results[Y, t][:].indirect(cen_t[:]))
+        def gather_centres(t, tag=None):
+            centres[t] = sbuf([P, V], F32, "centre%d" % t, tag)
+            window = results[Y, t][:].indirect(cen_t[:])
+            if t < 2:
+                nc.vector.tensor_copy(centres[t][:], window)
+            else:
+                nc.scalar.activation(centres[t][:], window, COPY)
 
         sums = [[sbuf([P, 2, V], F32, "%s_sum%d" % (name, d)) for d in range(2)] for name in ("first", "last")]
         acts = [sbuf([P, 2, V, 2], BF16, "act%d" % d) for d in range(2)]
@@ -213,7 +213,7 @@ def tile_picked_edgecv_gelu_p_kernel(
             nc.vector.quantize_mx(
                 out=z_codes[:].bitcast(FP8X4), scales=z_plane[:], in_=z_bf[:].rearrange("p v u e -> p (v u e)")
             )
-            acc = bank(FIRST_OUT_BANK + s, width)
+            acc = bank(OUT_BANKS[s], width)
             nc.tensor.matmul_mx(
                 out=acc[:],
                 lhsT=w3_codes[:].bitcast(FP8X4),
@@ -228,59 +228,61 @@ def tile_picked_edgecv_gelu_p_kernel(
             nc.sync.dma_start(out[:, lo:hi], staged[:])
 
 
+        pairs = (range(0, 2), range(2, 4))
         nc.vector.tensor_copy(x_plane[:], scale_table[:].indirect(offs_t[:]))
         gather_words(0)
-        round_pair(0, 0, nc.scalar.copy)
-        quantise(0, (0, 1))
-        round_with_gpsimd(0, 1, GPSIMD_SHARE_PART_0)
-        quantise(0, (2, 3))
+        round_hands(0, pairs[0], nc.scalar.copy)
+        quantise(0, 0, pairs[0])
+        round_on_gpsimd(0, pairs[1], GPSIMD_SHARE_PART_0)
+        round_hands(0, pairs[1], nc.scalar.copy, GPSIMD_SHARE_PART_0, P)
+        quantise(0, 2, pairs[1])
         gather_words(1)
         for t in range(3):
             multiply(Y, t, (0,))
-        round_with_vector(1, 0)
-        quantise(1, (0,))
-        quantise(1, (1,))
-        round_with_vector(1, 1)
-        quantise(1, (2, 3))
+        round_with_vector(1, pairs[0])
+        quantise(1, 0, range(0, 1))
+        quantise(1, 0, range(1, 2))
+        round_with_vector(1, pairs[1])
+        quantise(1, 2, pairs[1])
         for t in range(3):
             multiply(Y, t, (1,))
         evacuate(Y, 0)
 
 
         for rows in row_halves:
-            round_pair(2, 0, nc.vector.tensor_copy, rows=rows)
-        quantise(2, (0, 1))
+            round_hands(2, pairs[0], nc.vector.tensor_copy, rows=rows)
+        quantise(2, 0, pairs[0])
+        round_on_gpsimd(2, pairs[1], P // 2, "w_bf2_0")
         gather_centres(0)
         evacuate(Y, 1)
-        gather_centres(1)
         multiply(Y, 3, (0, 1))
         evacuate(Y, 2)
-        gather_centres(2)
-        evacuate(Y, 3)
-        round_with_gpsimd(3, 0, GPSIMD_SHARE_PART_3)
-        quantise(3, (0,))
-        quantise(3, (1,))
-        gather_centres(3)
-        round_pair(3, 1, nc.scalar.copy)
-        quantise(3, (2, 3), "result0_3")
+        round_hands(2, pairs[1], nc.scalar.copy, P // 2, P)
+        for pair in pairs:
+            round_hands(3, pair, nc.vector.tensor_copy)
+        quantise(3, 0, range(0, 1))
+        quantise(3, 0, range(1, 2))
+        quantise(3, 2, pairs[1])
+        gather_centres(1, "w_bf3_0")
 
 
-        for g in range(PASSES):
-            for t in (0, 1):
-                multiply(E, t, (g,))
-        for t in (2, 3):
-            multiply(E, t, (1,))
-        evacuate(E, 0, nc.vector.tensor_copy)
+        multiply(E, 0, (0,))
+        multiply(E, 0, (1,))
+        multiply(E, 1, (1, 0))
+        evacuate(E, 0)
+        quantise(2, 2, pairs[1], "w_codes3_0")
+        multiply(E, 2, (0, 1))
+        multiply(E, 3, (0, 1))
         for d in range(2):
             add_neighbours(0, d)
-        round_pair(2, 1, nc.scalar.copy, tag="w_codes3_0")
-        quantise(2, (2, 3))
         evacuate(E, 1)
+        gather_centres(2, "w_codes2_0")
+        evacuate(Y, 3, tag="w_codes3_1")
         for d in range(2):
             add_neighbours(1, d)
-        for t in (2, 3):
-            multiply(E, t, (0,))
-            evacuate(E, t)
+        evacuate(E, 2)
+        gather_centres(3)
+        evacuate(E, 3)
         for d in range(2):
             activate(0, d, 0, V)
         for d in range(2):

@@ -27,10 +27,19 @@ BANK = 512
 Y, E = 0, 1
 
 EARLY_COLUMNS = 3 * T // 8
+FETCHED = 3 * V // 8
 GPSIMD_SHARE_PART_0 = 5 * P // 8
+GPSIMD_SHARE_PART_2 = 5 * P // 8
+GPSIMD_SHARE_PART_3 = 5 * P // 8
+RING = {"centre1": 0, (3, 0): 768, (3, 2): 1024, (2, 0): 1280, (2, 2): 2048}
+HAND_STEP = {(3, 0): 2304}
+RING_WIDTH = 768 + 2 * 2304
 SLICES = (256, 128, 128)
-FIRST_BANK = {(Y, 0): 0, (Y, 1): 4, (Y, 2): 6, (Y, 3): 0, (E, 0): 2, (E, 1): 6, (E, 2): 2, (E, 3): 4}
-OUT_BANKS = (6, 7, 0)
+BANKS = {
+    (Y, 0): (0, 1), (Y, 1): (2, 3), (Y, 2): (4, 5), (Y, 3): (6, 7),
+    (E, 0): (0, 1), (E, 1): (2, 3), (E, 2): (4, 5), (E, 3): (6, 7),
+}
+OUT_BANKS = (0, 1, 2)
 
 
 def tile_picked_edgecv_gelu_p_kernel(
@@ -115,7 +124,16 @@ def tile_picked_edgecv_gelu_p_kernel(
         w_codes = {}
         w_plane = {}
 
+        ring = sbuf([P, RING_WIDTH], BF16, "ring")
+
+        def in_ring(key, width):
+            return ring[:, RING[key] : RING[key] + width]
+
         def rounded(part, hands, tag=None):
+            if (part, hands.start) in RING:
+                step = HAND_STEP.get((part, hands.start), P * PACK)
+                rows = in_ring((part, hands.start), len(hands) * step).rearrange("p (t x) -> p t x", x=step)
+                return rows[:, :, : P * PACK].rearrange("p t (m j) -> p t m j", j=PACK)
             if (part, hands.start) not in w_bf:
                 shape = [P, len(hands), P, PACK]
                 w_bf[part, hands.start] = sbuf(shape, BF16, "w_bf%d_%d" % (part, hands.start), tag)
@@ -127,8 +145,8 @@ def tile_picked_edgecv_gelu_p_kernel(
             copy(target[:, lo:hi, rows], source[:, lo:hi, rows])
 
         def round_on_gpsimd(part, hands, share=P, tag=None):
-            source = raw[part][:].rearrange("p j (m t) -> p t m j", t=PACK)[:, hands.start : hands.stop]
-            nc.gpsimd.tensor_copy(rounded(part, hands, tag)[:, :, :share], source[:, :, :share])
+            rounded(part, hands, tag)
+            round_hands(part, hands, nc.gpsimd.tensor_copy, 0, share)
 
         def round_with_vector(part, hands):
             round_hands(part, hands, nc.vector.tensor_copy, 0, P // 2)
@@ -137,7 +155,7 @@ def tile_picked_edgecv_gelu_p_kernel(
         def quantise(part, tile_start, hands, tag=None):
             codes = sbuf([P, len(hands) * P], U32, "w_codes%d_%d" % (part, hands.start), tag)
             plane = sbuf([P, len(hands) * P], U8, "w_plane%d_%d" % (part, hands.start))
-            values = w_bf[part, tile_start][:, hands.start - tile_start : hands.stop - tile_start]
+            values = rounded(part, range(tile_start, tile_start + 2))[:, hands.start - tile_start : hands.stop - tile_start]
             nc.vector.quantize_mx(
                 out=codes[:].bitcast(FP8X4), scales=plane[:], in_=values.rearrange("p t m j -> p (t m j)")
             )
@@ -148,16 +166,16 @@ def tile_picked_edgecv_gelu_p_kernel(
         accs = {}
         results = {}
 
-        def pieces_of(t):
-            width = BANK // 2 if t == 0 else BANK
+        def pieces_of(result, t):
+            width = BANK // len(BANKS[result, t]) * 2
             return [slice(lo, lo + width) for lo in range(0, S, width)]
 
-        def multiply(result, t, passes):
-            for piece, columns in enumerate(pieces_of(t)):
-                for g in passes:
+        def multiply(result, t, passes, only=None):
+            for piece, columns in enumerate(pieces_of(result, t)):
+                for g in passes if only in (None, piece) else ():
                     start = (result, t, piece) not in accs
                     if start:
-                        accs[result, t, piece] = bank(FIRST_BANK[result, t] + piece, columns.stop - columns.start)
+                        accs[result, t, piece] = bank(BANKS[result, t][piece], columns.stop - columns.start)
                     nc.tensor.matmul_mx(
                         out=accs[result, t, piece][:],
                         lhsT=w_codes[PASSES * result + g, t].bitcast(FP8X4),
@@ -168,16 +186,19 @@ def tile_picked_edgecv_gelu_p_kernel(
                         stop=not start,
                     )
 
-        def evacuate(result, t, first_copy=nc.scalar.copy, tag=None):
-            results[result, t] = sbuf([P, S], F32, "result%d_%d" % (result, t), tag)
-            for piece, columns in enumerate(pieces_of(t)):
-                copy = first_copy if piece == 0 else nc.scalar.copy
-                copy(results[result, t][:, columns], accs[result, t, piece][:])
+        def evacuate(result, t, only=None, last_copy=nc.scalar.copy):
+            if (result, t) not in results:
+                results[result, t] = sbuf([P, S], F32, "result%d_%d" % (result, t))
+            for piece, columns in enumerate(pieces_of(result, t)):
+                if only in (None, piece):
+                    copy = last_copy if columns.stop == S else nc.scalar.copy
+                    copy(results[result, t][:, columns], accs[result, t, piece][:])
 
         centres = {}
 
         def gather_centres(t, tag=None):
-            centres[t] = sbuf([P, V], F32, "centre%d" % t, tag)
+            name = "centre%d" % t
+            centres[t] = in_ring(name, 2 * V).bitcast(F32) if name in RING else sbuf([P, V], F32, name, tag)
             window = results[Y, t][:].indirect(cen_t[:])
             if t < 2:
                 nc.vector.tensor_copy(centres[t][:], window)
@@ -187,6 +208,8 @@ def tile_picked_edgecv_gelu_p_kernel(
         sums = [[sbuf([P, 2, V], F32, "%s_sum%d" % (name, d)) for d in range(2)] for name in ("first", "last")]
         acts = [sbuf([P, 2, V, 2], BF16, "act%d" % d) for d in range(2)]
 
+        fetched = sbuf([P, FETCHED], F32, "fetched")
+
         def add_neighbours(t, d, lo=0, hi=V):
             nc.vector.tensor_tensor(
                 sums[t // 2][d][:, t % 2, lo:hi],
@@ -194,6 +217,13 @@ def tile_picked_edgecv_gelu_p_kernel(
                 centres[t][:, lo:hi],
                 ADD,
             )
+
+        def fetch_neighbours(t, d, lo, hi):
+            window = results[E, t][:].indirect(pos_t[d][:, lo // LIST_ROWS : hi // LIST_ROWS])
+            nc.scalar.activation(fetched[:, lo:hi], window, COPY)
+
+        def add_centres(t, d, lo, hi):
+            nc.vector.tensor_tensor(sums[t // 2][d][:, t % 2, lo:hi], fetched[:, lo:hi], centres[t][:, lo:hi], ADD)
 
         def activate(u, d, lo, hi):
             source = sums[u][d][:, :, lo:hi].rearrange("p e v -> p v e")
@@ -237,51 +267,56 @@ def tile_picked_edgecv_gelu_p_kernel(
         round_hands(0, pairs[1], nc.scalar.copy, GPSIMD_SHARE_PART_0, P)
         quantise(0, 2, pairs[1])
         gather_words(1)
-        for t in range(3):
+        for t in range(PACK):
             multiply(Y, t, (0,))
         round_with_vector(1, pairs[0])
         quantise(1, 0, range(0, 1))
         quantise(1, 0, range(1, 2))
         round_with_vector(1, pairs[1])
         quantise(1, 2, pairs[1])
-        for t in range(3):
+        for t in range(PACK):
             multiply(Y, t, (1,))
         evacuate(Y, 0)
 
 
         for rows in row_halves:
             round_hands(2, pairs[0], nc.vector.tensor_copy, rows=rows)
-        quantise(2, 0, pairs[0])
-        round_on_gpsimd(2, pairs[1], P // 2, "w_bf2_0")
+        round_hands(2, pairs[1], nc.vector.tensor_copy, GPSIMD_SHARE_PART_2, P)
+        quantise(2, 0, range(1, 2))
+        quantise(2, 0, range(0, 1))
+        round_on_gpsimd(2, pairs[1], GPSIMD_SHARE_PART_2)
         gather_centres(0)
         evacuate(Y, 1)
-        multiply(Y, 3, (0, 1))
+        multiply(E, 0, (0,))
+        multiply(E, 1, (0,))
         evacuate(Y, 2)
-        round_hands(2, pairs[1], nc.scalar.copy, P // 2, P)
-        for pair in pairs:
-            round_hands(3, pair, nc.vector.tensor_copy)
+        evacuate(Y, 3)
+        round_hands(3, pairs[0], nc.vector.tensor_copy)
+        round_hands(3, pairs[1], nc.vector.tensor_copy, GPSIMD_SHARE_PART_3, P)
         quantise(3, 0, range(0, 1))
         quantise(3, 0, range(1, 2))
-        quantise(3, 2, pairs[1])
-        gather_centres(1, "w_bf3_0")
+        round_on_gpsimd(3, pairs[1], GPSIMD_SHARE_PART_3)
+        gather_centres(1)
 
 
-        multiply(E, 0, (0,))
         multiply(E, 0, (1,))
-        multiply(E, 1, (1, 0))
+        multiply(E, 1, (1,))
         evacuate(E, 0)
         quantise(2, 2, pairs[1], "w_codes3_0")
-        multiply(E, 2, (0, 1))
-        multiply(E, 3, (0, 1))
-        for d in range(2):
-            add_neighbours(0, d)
+        quantise(3, 2, pairs[1])
+        for g in range(PASSES):
+            multiply(E, 2, (g,))
+            multiply(E, 3, (g,))
+        fetch_neighbours(0, 1, 0, FETCHED)
+        add_neighbours(0, 0)
+        add_neighbours(0, 1, FETCHED, V)
+        add_centres(0, 1, 0, FETCHED)
         evacuate(E, 1)
-        gather_centres(2, "w_codes2_0")
-        evacuate(Y, 3, tag="w_codes3_1")
+        gather_centres(2, "w_codes3_1")
         for d in range(2):
             add_neighbours(1, d)
         evacuate(E, 2)
-        gather_centres(3)
+        gather_centres(3, "w_codes3_2")
         evacuate(E, 3)
         for d in range(2):
             activate(0, d, 0, V)

from contextlib import ExitStack

import concourse.mybir as mybir

K, T, S, V, H, N = 1024, 2048, 1024, 512, 512, 128
FLOPS = 2 * (2 * K * H * S + H * N * V)

F32 = mybir.dt.float32
BF16 = mybir.dt.bfloat16
I32 = mybir.dt.int32
U32 = mybir.dt.uint32
U16 = mybir.dt.uint16
U8 = mybir.dt.uint8
FP8X4 = mybir.dt.float8_e4m3fn_x4
GELU = mybir.ActivationFunctionType.Gelu_apprx_tanh
COPY = mybir.ActivationFunctionType.Copy
ADD = mybir.AluOpType.add
MAX = mybir.AluOpType.max

P = 128
PACK = 4
PASSES = K // (P * PACK)
QUADRANT = 32
PLANE_ROWS = 4
LIST_ROWS = 16
BANK = 512
Y, E = 0, 1

EARLY_COLUMNS = 3 * T // 8
FETCHED = 3 * V // 8
GPSIMD_SHARE_PART_0 = 5 * P // 8
GPSIMD_SHARE_PART_2 = 5 * P // 8
GPSIMD_SHARE_PART_3 = 5 * P // 8
RING = {"centre1": 0, (3, 0): 768, (3, 2): 1024, (2, 0): 1280, (2, 2): 2048}
HAND_STEP = {(3, 0): 2304}
RING_WIDTH = 768 + 2 * 2304
SLICES = (256, 128, 128)
BANKS = {
    (Y, 0): (0, 1), (Y, 1): (2, 3), (Y, 2): (4, 5), (Y, 3): (6, 7),
    (E, 0): (0, 1), (E, 1): (2, 3), (E, 2): (4, 5), (E, 3): (6, 7),
}
OUT_BANKS = (0, 1, 2)


def tile_picked_edgecv_gelu_p_kernel(
    tc, x_words, x_scales, w1, w2, w3_words, w3_scales, offs, cen, pos1, pos2, out
):
    nc = tc.nc
    with ExitStack() as ctx:
        keep = ctx.enter_context(tc.tile_pool(name="keep", bufs=1))
        psum = ctx.enter_context(tc.psum_pool(name="psum", bufs=1))

        def bank(index, width):
            return psum.tile([P, width], F32, name="bank%d" % index, tag="bank%d" % index)

        def sbuf(shape, dtype, name, tag=None):
            return keep.tile(shape, dtype, name=name, tag=tag or name, align_bytes=64)

        def load_list(source, name):
            tile = keep.tile(list(source.shape), U16, name=name)
            nc.sync.dma_start(tile[:], source)
            return tile


        scale_table = sbuf([P, T], U8, "scale_table")
        nc.vector.memset(scale_table[:, : T // 2].bitcast(I32), 0)
        nc.gpsimd.memset(scale_table[:, T // 2 :].bitcast(I32), 0)
        word_tables = [sbuf([P, T], I32, "word_table%d" % g) for g in range(PASSES)]

        def load_words(g, lo, hi):
            words = x_words[g].rearrange("p n t -> p (n t)").bitcast(I32)
            nc.sync.dma_start(word_tables[g][:, lo:hi], words[:, lo:hi])

        load_words(0, 0, EARLY_COLUMNS)
        offs_t = load_list(offs, "offs_t")
        for q in range(P // QUADRANT):
            nc.sync.dma_start(
                scale_table[QUADRANT * q : QUADRANT * q + PLANE_ROWS * PASSES, :].bitcast(I32),
                x_scales[:, PLANE_ROWS * q : PLANE_ROWS * (q + 1), :].bitcast(I32),
            )
        zero_in = keep.tile([P, 1], F32, name="zero_in")
        nc.vector.memset(zero_in[:], 0.0)
        zero_bias = keep.tile([P, 1], F32, name="zero_bias")
        nc.scalar.activation(zero_bias[:], zero_in[:], GELU)
        w3_plane = sbuf([P, N], U8, "w3_plane")
        nc.vector.memset(w3_plane[:].bitcast(I32), 0)

        raw = {}
        all_rows = slice(0, PACK)
        row_halves = (slice(0, PACK // 2), slice(PACK // 2, PACK))

        def load_part(part, pieces=(all_rows,)):
            w, g = (w1, w2)[part // PASSES], part % PASSES
            raw[part] = sbuf([P, PACK, H], F32, "raw%d" % part)
            source = w[g * P * PACK : (g + 1) * P * PACK, :].rearrange("(p j) c -> p j c", j=PACK)
            for rows in pieces:
                nc.sync.dma_start(raw[part][:, rows], source[:, rows])

        load_words(0, EARLY_COLUMNS, T)
        load_part(0)
        load_words(1, 0, T)
        load_part(1)
        load_part(2, row_halves)
        cen_t = load_list(cen, "cen_t")
        load_part(3)
        pos_t = [load_list(pos1, "pos1_t"), load_list(pos2, "pos2_t")]
        w3_codes = sbuf([P, N], I32, "w3_codes")
        nc.sync.dma_start(w3_codes[:], w3_words[0].rearrange("p n t -> p (n t)").bitcast(I32))
        for q in range(P // QUADRANT):
            nc.sync.dma_start(
                w3_plane[QUADRANT * q : QUADRANT * q + PLANE_ROWS, :].bitcast(I32),
                w3_scales[0, PLANE_ROWS * q : PLANE_ROWS * (q + 1), :].bitcast(I32),
            )


        x_plane = sbuf([P, S], U8, "x_plane")
        x_codes = {}

        def gather_words(g):
            x_codes[g] = sbuf([P, S], U32, "x_codes%d_0" % g)
            nc.vector.tensor_copy(x_codes[g][:], word_tables[g][:].bitcast(U32).indirect(offs_t[:]))

        w_bf = {}
        w_codes = {}
        w_plane = {}

        ring = sbuf([P, RING_WIDTH], BF16, "ring")

        def in_ring(key, width):
            return ring[:, RING[key] : RING[key] + width]

        def rounded(part, hands, tag=None):
            if (part, hands.start) in RING:
                step = HAND_STEP.get((part, hands.start), P * PACK)
                rows = in_ring((part, hands.start), len(hands) * step).rearrange("p (t x) -> p t x", x=step)
                return rows[:, :, : P * PACK].rearrange("p t (m j) -> p t m j", j=PACK)
            if (part, hands.start) not in w_bf:
                shape = [P, len(hands), P, PACK]
                w_bf[part, hands.start] = sbuf(shape, BF16, "w_bf%d_%d" % (part, hands.start), tag)
            return w_bf[part, hands.start]

        def round_hands(part, hands, copy, lo=0, hi=P, rows=all_rows):
            source = raw[part][:].rearrange("p j (m t) -> p m j t", t=PACK)[:, :, :, hands.start : hands.stop]
            target = rounded(part, hands)[:].rearrange("p t m j -> p m j t")
            copy(target[:, lo:hi, rows], source[:, lo:hi, rows])

        def round_on_gpsimd(part, hands, share=P, tag=None):
            rounded(part, hands, tag)
            round_hands(part, hands, nc.gpsimd.tensor_copy, 0, share)

        def round_with_vector(part, hands):
            round_hands(part, hands, nc.vector.tensor_copy, 0, P // 2)
            round_hands(part, hands, nc.scalar.copy, P // 2, P)

        def quantise(part, tile_start, hands, tag=None):
            codes = sbuf([P, len(hands) * P], U32, "w_codes%d_%d" % (part, hands.start), tag)
            plane = sbuf([P, len(hands) * P], U8, "w_plane%d_%d" % (part, hands.start))
            values = rounded(part, range(tile_start, tile_start + 2))[:, hands.start - tile_start : hands.stop - tile_start]
            nc.vector.quantize_mx(
                out=codes[:].bitcast(FP8X4), scales=plane[:], in_=values.rearrange("p t m j -> p (t m j)")
            )
            for place, t in enumerate(hands):
                w_codes[part, t] = codes[:, place * P : (place + 1) * P]
                w_plane[part, t] = plane[:, place * P : (place + 1) * P]

        accs = {}
        results = {}

        def pieces_of(result, t):
            width = BANK // len(BANKS[result, t]) * 2
            return [slice(lo, lo + width) for lo in range(0, S, width)]

        def multiply(result, t, passes, only=None):
            for piece, columns in enumerate(pieces_of(result, t)):
                for g in passes if only in (None, piece) else ():
                    start = (result, t, piece) not in accs
                    if start:
                        accs[result, t, piece] = bank(BANKS[result, t][piece], columns.stop - columns.start)
                    nc.tensor.matmul_mx(
                        out=accs[result, t, piece][:],
                        lhsT=w_codes[PASSES * result + g, t].bitcast(FP8X4),
                        lhsT_scale=w_plane[PASSES * result + g, t],
                        rhs=x_codes[g][:, columns].bitcast(FP8X4),
                        rhs_scale=x_plane[PLANE_ROWS * g :, columns],
                        start=start,
                        stop=not start,
                    )

        def evacuate(result, t, only=None, last_copy=nc.scalar.copy):
            if (result, t) not in results:
                results[result, t] = sbuf([P, S], F32, "result%d_%d" % (result, t))
            for piece, columns in enumerate(pieces_of(result, t)):
                if only in (None, piece):
                    copy = last_copy if columns.stop == S else nc.scalar.copy
                    copy(results[result, t][:, columns], accs[result, t, piece][:])

        centres = {}

        def gather_centres(t, tag=None):
            name = "centre%d" % t
            centres[t] = in_ring(name, 2 * V).bitcast(F32) if name in RING else sbuf([P, V], F32, name, tag)
            window = results[Y, t][:].indirect(cen_t[:])
            if t < 2:
                nc.vector.tensor_copy(centres[t][:], window)
            else:
                nc.scalar.activation(centres[t][:], window, COPY)

        sums = [[sbuf([P, 2, V], F32, "%s_sum%d" % (name, d)) for d in range(2)] for name in ("first", "last")]
        acts = [sbuf([P, 2, V, 2], BF16, "act%d" % d) for d in range(2)]

        fetched = sbuf([P, FETCHED], F32, "fetched")

        def add_neighbours(t, d, lo=0, hi=V):
            nc.vector.tensor_tensor(
                sums[t // 2][d][:, t % 2, lo:hi],
                results[E, t][:].indirect(pos_t[d][:, lo // LIST_ROWS : hi // LIST_ROWS]),
                centres[t][:, lo:hi],
                ADD,
            )

        def fetch_neighbours(t, d, lo, hi):
            window = results[E, t][:].indirect(pos_t[d][:, lo // LIST_ROWS : hi // LIST_ROWS])
            nc.scalar.activation(fetched[:, lo:hi], window, COPY)

        def add_centres(t, d, lo, hi):
            nc.vector.tensor_tensor(sums[t // 2][d][:, t % 2, lo:hi], fetched[:, lo:hi], centres[t][:, lo:hi], ADD)

        def activate(u, d, lo, hi):
            source = sums[u][d][:, :, lo:hi].rearrange("p e v -> p v e")
            nc.scalar.activation(acts[d][:, u, lo:hi], source, GELU, bias=zero_bias[:])

        def project(s, lo, hi):
            width = hi - lo
            z_bf = sbuf([P, width, 2, 2], BF16, "z_bf%d" % s)
            nc.vector.tensor_tensor(
                z_bf[:],
                acts[0][:, :, lo:hi].rearrange("p u v e -> p v u e"),
                acts[1][:, :, lo:hi].rearrange("p u v e -> p v u e"),
                MAX,
            )
            z_codes = sbuf([P, width], U32, "z_codes%d" % s)
            z_plane = sbuf([P, width], U8, "z_plane%d" % s)
            nc.vector.quantize_mx(
                out=z_codes[:].bitcast(FP8X4), scales=z_plane[:], in_=z_bf[:].rearrange("p v u e -> p (v u e)")
            )
            acc = bank(OUT_BANKS[s], width)
            nc.tensor.matmul_mx(
                out=acc[:],
                lhsT=w3_codes[:].bitcast(FP8X4),
                lhsT_scale=w3_plane[:],
                rhs=z_codes[:].bitcast(FP8X4),
                rhs_scale=z_plane[:],
                start=True,
                stop=True,
            )
            staged = sbuf([P, width], F32, "staged%d" % s)
            nc.scalar.copy(staged[:], acc[:])
            nc.sync.dma_start(out[:, lo:hi], staged[:])


        pairs = (range(0, 2), range(2, 4))
        nc.vector.tensor_copy(x_plane[:], scale_table[:].indirect(offs_t[:]))
        gather_words(0)
        round_hands(0, pairs[0], nc.scalar.copy)
        quantise(0, 0, pairs[0])
        round_on_gpsimd(0, pairs[1], GPSIMD_SHARE_PART_0)
        round_hands(0, pairs[1], nc.scalar.copy, GPSIMD_SHARE_PART_0, P)
        quantise(0, 2, pairs[1])
        gather_words(1)
        for t in range(PACK):
            multiply(Y, t, (0,))
        round_with_vector(1, pairs[0])
        quantise(1, 0, range(0, 1))
        quantise(1, 0, range(1, 2))
        round_with_vector(1, pairs[1])
        quantise(1, 2, pairs[1])
        for t in range(PACK):
            multiply(Y, t, (1,))
        evacuate(Y, 0)


        for rows in row_halves:
            round_hands(2, pairs[0], nc.vector.tensor_copy, rows=rows)
        round_hands(2, pairs[1], nc.vector.tensor_copy, GPSIMD_SHARE_PART_2, P)
        quantise(2, 0, range(1, 2))
        quantise(2, 0, range(0, 1))
        round_on_gpsimd(2, pairs[1], GPSIMD_SHARE_PART_2)
        gather_centres(0)
        evacuate(Y, 1)
        multiply(E, 0, (0,))
        multiply(E, 1, (0,))
        evacuate(Y, 2)
        evacuate(Y, 3)
        round_hands(3, pairs[0], nc.vector.tensor_copy)
        round_hands(3, pairs[1], nc.vector.tensor_copy, GPSIMD_SHARE_PART_3, P)
        quantise(3, 0, range(0, 1))
        quantise(3, 0, range(1, 2))
        round_on_gpsimd(3, pairs[1], GPSIMD_SHARE_PART_3)
        gather_centres(1)


        multiply(E, 0, (1,))
        multiply(E, 1, (1,))
        evacuate(E, 0)
        quantise(2, 2, pairs[1], "w_codes3_0")
        quantise(3, 2, pairs[1])
        for g in range(PASSES):
            multiply(E, 2, (g,))
            multiply(E, 3, (g,))
        fetch_neighbours(0, 1, 0, FETCHED)
        add_neighbours(0, 0)
        add_neighbours(0, 1, FETCHED, V)
        add_centres(0, 1, 0, FETCHED)
        evacuate(E, 1)
        gather_centres(2, "w_codes3_1")
        for d in range(2):
            add_neighbours(1, d)
        evacuate(E, 2)
        gather_centres(3, "w_codes3_2")
        evacuate(E, 3)
        for d in range(2):
            activate(0, d, 0, V)
        for d in range(2):
            add_neighbours(2, d)


        half = V // 2
        for lo in (0, half):
            for d in range(2):
                add_neighbours(3, d, lo, lo + half)
        for d in range(2):
            activate(1, d, 0, half)
        activate(1, 0, half, V)
        bounds = [(sum(SLICES[:s]), sum(SLICES[: s + 1])) for s in range(len(SLICES))]
        for lo, hi in bounds[1:]:
            activate(1, 1, lo, hi)
        for s, (lo, hi) in enumerate(bounds):
            project(s, lo, hi)
